import numpy as np
import ml_dtypes


def mxq(x, axis, fmt="e4m3"):
    dtype, down = {"e4m3": (ml_dtypes.float8_e4m3fn, 7), "e5m2": (ml_dtypes.float8_e5m2, 14)}[fmt]
    v = np.moveaxis(np.asarray(x, np.float32).astype(ml_dtypes.bfloat16).astype(np.float64), axis, -1)
    blocks = v.reshape(v.shape[:-1] + (-1, 32))
    amax = np.abs(blocks).max(-1, keepdims=True)
    byte = np.maximum(np.where(amax > 0, np.frexp(amax)[1] - 1 + 127, 0) - down, 1)
    scale = np.exp2(byte - 127.0)
    codes = (blocks / scale).astype(np.float32).astype(dtype).astype(np.float64)
    return np.moveaxis((codes * scale).reshape(v.shape), -1, axis)


WIDE = False


def mx_kscale(k):
    if not WIDE:
        return np.ones(k)
    levels = np.array([10, -10, 5, -5, 0])
    if k % 512:
        return np.exp2(np.random.permutation(np.resize(levels, k // 32))).repeat(32)
    a = np.empty((k // 512, 16))
    for p in range(k // 512):
        a[p, :8] = np.random.permutation(np.resize(levels, 8))
        for g in range(8):
            far = levels[np.abs(levels - a[p, g]) >= 10]
            a[p, g + 8] = far[np.random.randint(len(far))]
    return np.exp2(a.ravel()).repeat(32)


def f64(x):
    return np.asarray(x).astype(np.float64)


def striped(idx):
    return np.tile(idx.reshape(-1, 16).T, (8, 1)).astype(np.uint16)


def unstriped(offs):
    return offs[:16].T.reshape(-1).astype(np.int64)


def pack_weight(w):
    k, n = w.shape
    w = f64(np.asarray(w, np.float32).astype(ml_dtypes.bfloat16)).reshape(k // 32, 32, n)
    amax = np.abs(w).max(1)
    byte = np.clip(np.where(amax > 0, np.frexp(amax)[1] - 1 + 127 - 7, 1), 1, 254)
    scaled = (w * np.exp2(127.0 - byte)[:, None, :]).reshape(k, n).astype(np.float32)
    words = np.ascontiguousarray(scaled.reshape(k // 512, 128, 4, n).transpose(0, 1, 3, 2)).astype(ml_dtypes.float8_e4m3fn).view(np.uint8)
    return words, np.ascontiguousarray(byte.astype(np.uint8).reshape(k // 512, 16, n))


def unpack_weight(words, scales):
    g, p, n, _ = words.shape
    vals = np.ascontiguousarray(words).view(ml_dtypes.float8_e4m3fn).astype(np.float64) * np.repeat(np.exp2(scales.astype(np.float64) - 127.0), 8, axis=1)[..., None]
    return vals.transpose(0, 1, 3, 2).reshape(g * 512, n)


def planes(y):
    n, m = y.shape
    v = y.astype(np.float32).astype(ml_dtypes.bfloat16).astype(np.float64).reshape(n // 32, 32, m)
    top = np.abs(v).max(1)
    byte = np.clip(np.where(top > 0, np.frexp(top)[1] - 1 + 127 - 7, 1), 1, 254)
    codes = (v * np.exp2(127.0 - byte)[:, None, :]).reshape(n, m).astype(np.float32).astype(ml_dtypes.float8_e4m3fn).view(np.uint8)
    words = codes.reshape(n // 512, 128, 4, m).transpose(0, 1, 3, 2)
    return np.ascontiguousarray(words), np.ascontiguousarray(byte.astype(np.uint8).reshape(n // 512, 16, m))


def relu(v):
    return np.maximum(v, 0.0)


K, T, S, H, N = 512, 2048, 512, 512, 512


def setup_inputs():
    n = np.random.standard_normal
    s = mx_kscale(K)[:, None]
    u = mx_kscale(H)
    packed_xT = pack_weight(n((K, T)) * s)
    return {
        "x_words": packed_xT[0],
        "x_scales": packed_xT[1],
        "mask": (n((N, T))).astype(np.float32),
        "w1": (n((K, H)) / np.sqrt(K) / s * u).astype(np.float32),
        "w2": (n((H, N)) / np.sqrt(H) / u[:, None]).astype(np.float32),
        "offs": striped(np.random.permutation(T)[:S]),
    }


def reference(x_words, x_scales, mask, w1, w2, offs):
    xq = unpack_weight(x_words, x_scales)[:, unstriped(offs)]
    h = relu(mxq(f64(w1), 0, "e4m3").T @ xq)
    y = mxq(f64(w2), 0, "e4m3").T @ mxq(h, 0, "e4m3")
    out = f64(mask).copy()
    out[:, unstriped(offs)] = y
    out_0 = out
    return (out_0,) + planes(out_0)

@@ -1,0 +1,215 @@
+from contextlib import ExitStack
+
+import concourse.mybir as mybir
+
+K, T, S, H, N = 512, 2048, 512, 512, 512
+FLOPS = 2 * K * H * S + 2 * H * N * S
+
+F32 = mybir.dt.float32
+BF16 = mybir.dt.bfloat16
+I32 = mybir.dt.int32
+U32 = mybir.dt.uint32
+U16 = mybir.dt.uint16
+U8 = mybir.dt.uint8
+FP8X4 = mybir.dt.float8_e4m3fn_x4
+RELU = mybir.ActivationFunctionType.Relu
+
+P = 128
+PACK = 4
+QUADS = 4
+ALIGN = 64
+HALF = S // 2
+N1 = 128
+CHUNK = 256
+N_CHUNKS = T // CHUNK
+SCALAR_WEAVES = 2
+STORE_CHUNKS = 2
+W1_SPLIT = 88
+
+
+def deal_weights(copy, grouped, raw, m0, m1, j0, j1):
+    copy(
+        out=grouped[:].rearrange("p (t m j) -> p m j t", t=PACK, j=PACK)[:, m0:m1, j0:j1],
+        in_=raw[:].rearrange("p (j m t) -> p m j t", j=j1 - j0, t=PACK)[:, m0:m1],
+    )
+
+
+def tile_picked_zmae_mlprelu_po_kernel(
+    tc, x_words, x_scales, mask, w1, w2, offs, out_0, out_1, out_2
+):
+    nc = tc.nc
+    mask_rows = mask.rearrange("(p t) c -> p t c", t=PACK)
+    out_rows = out_0.rearrange("(p t) c -> p t c", t=PACK)
+    out_words = out_1[0].rearrange("p c r -> p (c r)").bitcast(I32)
+
+    with ExitStack() as ctx:
+        keep = ctx.enter_context(tc.tile_pool(name="keep", bufs=1))
+        psum = ctx.enter_context(tc.psum_pool(name="psum", bufs=8))
+
+        offsets = keep.tile([P, S // 16], U16, name="offsets")
+        nc.sync.dma_start(offsets[:], offs)
+
+        w1_raw = keep.tile([P, PACK * H], F32, name="w1_raw", tag="slot0", align_bytes=ALIGN)
+        nc.sync.dma_start(w1_raw[:], w1.rearrange("(p j) c -> p (j c)", j=PACK))
+
+        scale_table = keep.tile([P, T], U8, name="scale_table", tag="slot1", align_bytes=ALIGN)
+        nc.vector.memset(scale_table[:].bitcast(I32), 0)
+        for q in range(QUADS):
+            nc.scalar.dma_start(
+                scale_table[32 * q : 32 * q + 4, :].bitcast(I32),
+                x_scales[0, 4 * q : 4 * q + 4, :].bitcast(I32),
+            )
+
+        word_table = keep.tile([P, T], I32, name="word_table", tag="slot2", align_bytes=ALIGN)
+        nc.sync.dma_start(word_table[:], x_words[0].rearrange("p c r -> p (c r)").bitcast(I32))
+
+        w2_rows = w2.rearrange("(p j) c -> p (j c)", j=PACK)
+        w2_first = keep.tile([P, 2 * N], F32, name="w2_first", tag="slot3", align_bytes=ALIGN)
+        nc.sync.dma_start(w2_first[:], w2_rows[:, : 2 * N])
+
+        x_scale = keep.tile([P, S], U8, name="x_scale", align_bytes=ALIGN)
+        nc.vector.tensor_copy(x_scale[:], scale_table[:].indirect(offsets[:]))
+
+        w1_grouped = keep.tile([P, PACK * H], BF16, name="w1_grouped", tag="slot1", align_bytes=ALIGN)
+        deal_weights(nc.vector.tensor_copy, w1_grouped, w1_raw, 0, W1_SPLIT, 0, PACK)
+        deal_weights(nc.scalar.copy, w1_grouped, w1_raw, W1_SPLIT, P, 0, PACK)
+        w2_second = keep.tile([P, 2 * N], F32, name="w2_second", tag="slot0", align_bytes=ALIGN)
+        nc.sync.dma_start(w2_second[:], w2_rows[:, 2 * N :])
+        w1_codes = keep.tile([P, H], U32, name="w1_codes", align_bytes=ALIGN)
+        w1_scale = keep.tile([P, H], U8, name="w1_scale", align_bytes=ALIGN)
+        nc.vector.quantize_mx(out=w1_codes[:].bitcast(FP8X4), scales=w1_scale[:], in_=w1_grouped[:])
+
+        x_codes = []
+        for a in range(2):
+            picked = keep.tile([P, HALF], U32, name=f"x_codes{a}", align_bytes=ALIGN)
+            cols = slice(a * HALF // 16, (a + 1) * HALF // 16)
+            nc.vector.tensor_copy(picked[:], word_table[:].bitcast(U32).indirect(offsets[:, cols]))
+            x_codes.append(picked)
+
+        w2_grouped = keep.tile([P, PACK * N], BF16, name="w2_grouped", align_bytes=ALIGN)
+        deal_weights(nc.vector.tensor_copy, w2_grouped, w2_first, 0, P, 0, 2)
+        deal_weights(nc.vector.tensor_copy, w2_grouped, w2_second, 0, P, 2, PACK)
+
+        windows = []
+        for t in range(PACK):
+            window = keep.tile([P, T], F32, name=f"window{t}", tag=f"slot{(t + 1) % PACK}", align_bytes=ALIGN)
+            nc.sync.dma_start(window[:], mask_rows[:, t, :])
+            windows.append(window)
+
+        h_grouped = [
+            keep.tile([P, HALF * PACK], BF16, name=f"h_grouped{a}", align_bytes=ALIGN) for a in range(2)
+        ]
+        for c in range(S // N1):
+            a, c0 = divmod(c * N1, HALF)
+            bank = psum.tile([P, PACK, N1], F32, name="bank", tag="bank")
+            for t in range(PACK):
+                nc.tensor.matmul_mx(
+                    out=bank[:, t, :],
+                    lhsT=w1_codes[:, t * P : (t + 1) * P].bitcast(FP8X4),
+                    lhsT_scale=w1_scale[:, t * P : (t + 1) * P],
+                    rhs=x_codes[a][:, c0 : c0 + N1].bitcast(FP8X4),
+                    rhs_scale=x_scale[:, c * N1 : (c + 1) * N1],
+                    start=True,
+                    stop=True,
+                )
+            nc.scalar.activation(
+                out=h_grouped[a][:, c0 * PACK : (c0 + N1) * PACK].rearrange("p (n t) -> p n t", t=PACK),
+                in_=bank[:].rearrange("p t n -> p n t"),
+                func=RELU,
+            )
+
+        h_codes = keep.tile([P, S], U32, name="h_codes", align_bytes=ALIGN)
+        h_scale = keep.tile([P, S], U8, name="h_scale", align_bytes=ALIGN)
+        w2_codes = keep.tile([P, N], U32, name="w2_codes", align_bytes=ALIGN)
+        w2_scale = keep.tile([P, N], U8, name="w2_scale", align_bytes=ALIGN)
+
+        def quantize_h(a):
+            cols = slice(a * HALF, (a + 1) * HALF)
+            nc.vector.quantize_mx(out=h_codes[:, cols].bitcast(FP8X4), scales=h_scale[:, cols], in_=h_grouped[a][:])
+
+        def quantize_w2(c0, c1):
+            nc.vector.quantize_mx(
+                out=w2_codes[:, c0:c1].bitcast(FP8X4),
+                scales=w2_scale[:, c0:c1],
+                in_=w2_grouped[:, c0 * PACK : c1 * PACK],
+            )
+
+        quantize_h(0)
+        quantize_w2(0, N // 2)
+        quantize_h(1)
+        quantize_w2(N // 2, N)
+
+        ys = []
+        for t in range(PACK):
+            y = keep.tile([P, S], F32, name=f"y{t}", align_bytes=ALIGN)
+            width = HALF if t == 0 else S
+            for c0 in range(0, S, width):
+                cols = slice(c0, c0 + width)
+                bank = psum.tile([P, width], F32, name="bank", tag="bank")
+                nc.tensor.matmul_mx(
+                    out=bank[:],
+                    lhsT=w2_codes[:, t * P : (t + 1) * P].bitcast(FP8X4),
+                    lhsT_scale=w2_scale[:, t * P : (t + 1) * P],
+                    rhs=h_codes[:, cols].bitcast(FP8X4),
+                    rhs_scale=h_scale[:, cols],
+                    start=True,
+                    stop=True,
+                )
+                nc.scalar.copy(out=y[:, cols], in_=bank[:])
+            ys.append(y)
+
+        pairs = [
+            keep.tile([P, 2, CHUNK, 2], BF16, name=f"pairs{c}", align_bytes=ALIGN) for c in range(N_CHUNKS)
+        ]
+
+        def round_plane(copy, t, c):
+            copy(out=pairs[c][:, t // 2, :, t % 2], in_=windows[t][:, c * CHUNK : (c + 1) * CHUNK])
+
+        for t in range(PACK):
+            nc.vector.tensor_copy(windows[t][:].indirect(offsets[:]), ys[t][:])
+            nc.sync.dma_start(out_rows[:, t, :], windows[t][:])
+            for c in range(0 if t < 2 else 1, N_CHUNKS):
+                round_plane(nc.scalar.copy, t, c)
+
+        out_scale = keep.tile([P, T // QUADS], U8, name="out_scale", align_bytes=ALIGN)
+        grouped = [
+            keep.tile([P, CHUNK * PACK], BF16, name=f"grouped{c}", align_bytes=ALIGN) for c in range(N_CHUNKS)
+        ]
+        store_width = STORE_CHUNKS * CHUNK
+        codes = [
+            keep.tile([P, store_width], I32, name=f"codes{s}", align_bytes=ALIGN) for s in range(T // store_width)
+        ]
+
+        def weave(copy, c):
+            copy(
+                out=grouped[c][:].bitcast(F32).rearrange("p (c u) -> p c u", u=2),
+                in_=pairs[c][:].rearrange("p u c e -> p u (c e)").bitcast(F32).rearrange("p u c -> p c u"),
+            )
+
+        def quantize_out(c):
+            s, r = divmod(c, STORE_CHUNKS)
+            nc.vector.quantize_mx(
+                out=codes[s][:, r * CHUNK : (r + 1) * CHUNK].bitcast(FP8X4),
+                scales=out_scale[4 * s :, r * CHUNK : (r + 1) * CHUNK],
+                in_=grouped[c][:],
+            )
+            if r == STORE_CHUNKS - 1:
+                nc.sync.dma_start(out_words[:, s * store_width : (s + 1) * store_width], codes[s][:])
+
+        vector_weaves = N_CHUNKS - SCALAR_WEAVES
+        for c in range(vector_weaves, N_CHUNKS):
+            weave(nc.scalar.copy, c)
+        round_plane(nc.vector.tensor_copy, 3, 0)
+        round_plane(nc.vector.tensor_copy, 2, 0)
+        for step in range(N_CHUNKS + 1):
+            if step < vector_weaves:
+                weave(nc.vector.tensor_copy, step)
+            if step >= 1:
+                quantize_out(step - 1)
+
+        for q in range(QUADS):
+            queue = nc.scalar if q % 2 else nc.sync
+            queue.dma_start(
+                out_2[0, 4 * q : 4 * q + 4, :].bitcast(I32).rearrange("r (s c) -> s r c", s=QUADS),
+                out_scale[32 * q : 32 * q + 16, :].bitcast(I32),
+            )

@@ -49,32 +49,32 @@ def tile_picked_zmae_mlprelu_po_kernel(
         offsets = keep.tile([P, S // 16], U16, name="offsets")
         nc.sync.dma_start(offsets[:], offs)
 
-        w1_raw = keep.tile([P, PACK * H], F32, name="w1_raw", tag="slot0", align_bytes=ALIGN)
-        nc.sync.dma_start(w1_raw[:], w1.rearrange("(p j) c -> p (j c)", j=PACK))
-
-        scale_table = keep.tile([P, T], U8, name="scale_table", tag="slot1", align_bytes=ALIGN)
+        scale_rows = keep.tile([P, T], U8, name="scale_rows", align_bytes=ALIGN)
+        scale_table = keep.tile([P, T], U8, name="scale_table", align_bytes=ALIGN)
         nc.vector.memset(scale_table[:].bitcast(I32), 0)
         for q in range(QUADS):
-            nc.scalar.dma_start(
-                scale_table[32 * q : 32 * q + 4, :].bitcast(I32),
-                x_scales[0, 4 * q : 4 * q + 4, :].bitcast(I32),
-            )
+            rows = slice(32 * q, 32 * q + 4)
+            nc.sync.dma_start(scale_rows[rows, :].bitcast(I32), x_scales[0, 4 * q : 4 * q + 4, :].bitcast(I32))
+            nc.vector.tensor_copy(scale_table[rows, :].bitcast(I32), scale_rows[rows, :].bitcast(I32))
 
-        word_table = keep.tile([P, T], I32, name="word_table", tag="slot2", align_bytes=ALIGN)
+        w1_raw = keep.tile([P, PACK * H], F32, name="w1_raw", align_bytes=ALIGN)
+        nc.sync.dma_start(w1_raw[:], w1.rearrange("(p j) c -> p (j c)", j=PACK))
+
+        word_table = keep.tile([P, T], I32, name="word_table", align_bytes=ALIGN)
         nc.sync.dma_start(word_table[:], x_words[0].rearrange("p c r -> p (c r)").bitcast(I32))
 
         w2_rows = w2.rearrange("(p j) c -> p (j c)", j=PACK)
-        w2_first = keep.tile([P, 2 * N], F32, name="w2_first", tag="slot3", align_bytes=ALIGN)
+        w2_first = keep.tile([P, 2 * N], F32, name="w2_first", align_bytes=ALIGN)
         nc.sync.dma_start(w2_first[:], w2_rows[:, : 2 * N])
+        w2_second = keep.tile([P, 2 * N], F32, name="w2_second", align_bytes=ALIGN)
+        nc.sync.dma_start(w2_second[:], w2_rows[:, 2 * N :])
 
         x_scale = keep.tile([P, S], U8, name="x_scale", align_bytes=ALIGN)
         nc.vector.tensor_copy(x_scale[:], scale_table[:].indirect(offsets[:]))
 
-        w1_grouped = keep.tile([P, PACK * H], BF16, name="w1_grouped", tag="slot1", align_bytes=ALIGN)
+        w1_grouped = keep.tile([P, PACK * H], BF16, name="w1_grouped", align_bytes=ALIGN)
         deal_weights(nc.vector.tensor_copy, w1_grouped, w1_raw, 0, W1_SPLIT, 0, PACK)
         deal_weights(nc.scalar.copy, w1_grouped, w1_raw, W1_SPLIT, P, 0, PACK)
-        w2_second = keep.tile([P, 2 * N], F32, name="w2_second", tag="slot0", align_bytes=ALIGN)
-        nc.sync.dma_start(w2_second[:], w2_rows[:, 2 * N :])
         w1_codes = keep.tile([P, H], U32, name="w1_codes", align_bytes=ALIGN)
         w1_scale = keep.tile([P, H], U8, name="w1_scale", align_bytes=ALIGN)
         nc.vector.quantize_mx(out=w1_codes[:].bitcast(FP8X4), scales=w1_scale[:], in_=w1_grouped[:])
@@ -92,7 +92,7 @@ def tile_picked_zmae_mlprelu_po_kernel(
 
         windows = []
         for t in range(PACK):
-            window = keep.tile([P, T], F32, name=f"window{t}", tag=f"slot{(t + 1) % PACK}", align_bytes=ALIGN)
+            window = keep.tile([P, T], F32, name=f"window{t}", align_bytes=ALIGN)
             nc.sync.dma_start(window[:], mask_rows[:, t, :])
             windows.append(window)
 
@@ -166,7 +166,10 @@ def tile_picked_zmae_mlprelu_po_kernel(
             copy(out=pairs[c][:, t // 2, :, t % 2], in_=windows[t][:, c * CHUNK : (c + 1) * CHUNK])
 
         for t in range(PACK):
-            nc.vector.tensor_copy(windows[t][:].indirect(offsets[:]), ys[t][:])
+            width = HALF if t == 0 else S
+            for c0 in range(0, S, width):
+                entries = offsets[:, c0 // 16 : (c0 + width) // 16]
+                nc.vector.tensor_copy(windows[t][:].indirect(entries), ys[t][:, c0 : c0 + width])
             nc.sync.dma_start(out_rows[:, t, :], windows[t][:])
             for c in range(0 if t < 2 else 1, N_CHUNKS):
                 round_plane(nc.scalar.copy, t, c)
@@ -208,7 +211,7 @@ def tile_picked_zmae_mlprelu_po_kernel(
                 quantize_out(step - 1)
 
         for q in range(QUADS):
-            queue = nc.scalar if q % 2 else nc.sync
+            queue = nc.sync if q == QUADS - 1 else nc.scalar
             queue.dma_start(
                 out_2[0, 4 * q : 4 * q + 4, :].bitcast(I32).rearrange("r (s c) -> s r c", s=QUADS),
                 out_scale[32 * q : 32 * q + 16, :].bitcast(I32),

@@ -24,7 +24,8 @@ CHUNK = 256
 N_CHUNKS = T // CHUNK
 SCALAR_WEAVES = 2
 STORE_CHUNKS = 2
-W1_SPLIT = 88
+W1_SPLIT = 80
+W2_SPLIT = 80
 
 
 def deal_weights(copy, grouped, raw, m0, m1, j0, j1):
@@ -72,22 +73,21 @@ def tile_picked_zmae_mlprelu_po_kernel(
         x_scale = keep.tile([P, S], U8, name="x_scale", align_bytes=ALIGN)
         nc.vector.tensor_copy(x_scale[:], scale_table[:].indirect(offsets[:]))
 
-        w1_grouped = keep.tile([P, PACK * H], BF16, name="w1_grouped", align_bytes=ALIGN)
+        w1_grouped = keep.tile([P, PACK * H], BF16, name="w1_grouped", tag="x_codes", align_bytes=ALIGN)
         deal_weights(nc.vector.tensor_copy, w1_grouped, w1_raw, 0, W1_SPLIT, 0, PACK)
         deal_weights(nc.scalar.copy, w1_grouped, w1_raw, W1_SPLIT, P, 0, PACK)
         w1_codes = keep.tile([P, H], U32, name="w1_codes", align_bytes=ALIGN)
         w1_scale = keep.tile([P, H], U8, name="w1_scale", align_bytes=ALIGN)
         nc.vector.quantize_mx(out=w1_codes[:].bitcast(FP8X4), scales=w1_scale[:], in_=w1_grouped[:])
 
-        x_codes = []
+        x_codes = keep.tile([P, S], U32, name="x_codes", tag="x_codes", align_bytes=ALIGN)
         for a in range(2):
-            picked = keep.tile([P, HALF], U32, name=f"x_codes{a}", align_bytes=ALIGN)
-            cols = slice(a * HALF // 16, (a + 1) * HALF // 16)
-            nc.vector.tensor_copy(picked[:], word_table[:].bitcast(U32).indirect(offsets[:, cols]))
-            x_codes.append(picked)
+            entries = offsets[:, a * HALF // 16 : (a + 1) * HALF // 16]
+            nc.vector.tensor_copy(x_codes[:, a * HALF : (a + 1) * HALF], word_table[:].bitcast(U32).indirect(entries))
 
         w2_grouped = keep.tile([P, PACK * N], BF16, name="w2_grouped", align_bytes=ALIGN)
-        deal_weights(nc.vector.tensor_copy, w2_grouped, w2_first, 0, P, 0, 2)
+        deal_weights(nc.scalar.copy, w2_grouped, w2_first, W2_SPLIT, P, 0, 2)
+        deal_weights(nc.vector.tensor_copy, w2_grouped, w2_first, 0, W2_SPLIT, 0, 2)
         deal_weights(nc.vector.tensor_copy, w2_grouped, w2_second, 0, P, 2, PACK)
 
         windows = []
@@ -107,7 +107,7 @@ def tile_picked_zmae_mlprelu_po_kernel(
                     out=bank[:, t, :],
                     lhsT=w1_codes[:, t * P : (t + 1) * P].bitcast(FP8X4),
                     lhsT_scale=w1_scale[:, t * P : (t + 1) * P],
-                    rhs=x_codes[a][:, c0 : c0 + N1].bitcast(FP8X4),
+                    rhs=x_codes[:, c * N1 : (c + 1) * N1].bitcast(FP8X4),
                     rhs_scale=x_scale[:, c * N1 : (c + 1) * N1],
                     start=True,
                     stop=True,

@@ -21,17 +21,21 @@ ALIGN = 64
 HALF = S // 2
 N1 = 128
 CHUNK = 256
-N_CHUNKS = T // CHUNK
-SCALAR_WEAVES = 2
-STORE_CHUNKS = 2
+EDGE = CHUNK // 2
+WIDTHS = [EDGE, EDGE] + [CHUNK] * (T // CHUNK - 2) + [EDGE, EDGE]
+STARTS = [sum(WIDTHS[:c]) for c in range(len(WIDTHS))]
+N_CHUNKS = len(WIDTHS)
+VECTOR_ROUNDS = 2
+SCALAR_WEAVES = 3
+QUARTER = T // QUADS
+STORE_ENDS = [QUARTER, 2 * QUARTER, 3 * QUARTER, T - CHUNK, T]
 W1_SPLIT = 80
-W2_SPLIT = 80
 
 
-def deal_weights(copy, grouped, raw, m0, m1, j0, j1):
+def deal_weights(copy, grouped, m0, m1, raw, first):
     copy(
-        out=grouped[:].rearrange("p (t m j) -> p m j t", t=PACK, j=PACK)[:, m0:m1, j0:j1],
-        in_=raw[:].rearrange("p (j m t) -> p m j t", j=j1 - j0, t=PACK)[:, m0:m1],
+        out=grouped[:].rearrange("p (t m j) -> p m j t", t=PACK, j=PACK)[:, m0:m1],
+        in_=raw[:].rearrange("p (j m t) -> p m j t", j=PACK, t=PACK)[:, m0 - first : m1 - first],
     )
 
 
@@ -55,27 +59,28 @@ def tile_picked_zmae_mlprelu_po_kernel(
         nc.vector.memset(scale_table[:].bitcast(I32), 0)
         for q in range(QUADS):
             rows = slice(32 * q, 32 * q + 4)
-            nc.sync.dma_start(scale_rows[rows, :].bitcast(I32), x_scales[0, 4 * q : 4 * q + 4, :].bitcast(I32))
+            queue = nc.sync if q < 2 else nc.scalar
+            queue.dma_start(scale_rows[rows, :].bitcast(I32), x_scales[0, 4 * q : 4 * q + 4, :].bitcast(I32))
             nc.vector.tensor_copy(scale_table[rows, :].bitcast(I32), scale_rows[rows, :].bitcast(I32))
 
         w1_raw = keep.tile([P, PACK * H], F32, name="w1_raw", align_bytes=ALIGN)
         nc.sync.dma_start(w1_raw[:], w1.rearrange("(p j) c -> p (j c)", j=PACK))
 
-        word_table = keep.tile([P, T], I32, name="word_table", align_bytes=ALIGN)
+        word_table = keep.tile([P, T], I32, name="word_table", tag="word_table", align_bytes=ALIGN)
         nc.sync.dma_start(word_table[:], x_words[0].rearrange("p c r -> p (c r)").bitcast(I32))
 
-        w2_rows = w2.rearrange("(p j) c -> p (j c)", j=PACK)
+        w2_rows = w2.rearrange("(p j) c -> p j c", j=PACK)
         w2_first = keep.tile([P, 2 * N], F32, name="w2_first", align_bytes=ALIGN)
-        nc.sync.dma_start(w2_first[:], w2_rows[:, : 2 * N])
+        nc.sync.dma_start(w2_first[:].rearrange("p (j c) -> p j c", j=PACK), w2_rows[:, :, : N // 2])
         w2_second = keep.tile([P, 2 * N], F32, name="w2_second", align_bytes=ALIGN)
-        nc.sync.dma_start(w2_second[:], w2_rows[:, 2 * N :])
+        nc.sync.dma_start(w2_second[:].rearrange("p (j c) -> p j c", j=PACK), w2_rows[:, :, N // 2 :])
 
         x_scale = keep.tile([P, S], U8, name="x_scale", align_bytes=ALIGN)
         nc.vector.tensor_copy(x_scale[:], scale_table[:].indirect(offsets[:]))
 
         w1_grouped = keep.tile([P, PACK * H], BF16, name="w1_grouped", tag="x_codes", align_bytes=ALIGN)
-        deal_weights(nc.vector.tensor_copy, w1_grouped, w1_raw, 0, W1_SPLIT, 0, PACK)
-        deal_weights(nc.scalar.copy, w1_grouped, w1_raw, W1_SPLIT, P, 0, PACK)
+        deal_weights(nc.vector.tensor_copy, w1_grouped, 0, W1_SPLIT, w1_raw, 0)
+        deal_weights(nc.scalar.copy, w1_grouped, W1_SPLIT, P, w1_raw, 0)
         w1_codes = keep.tile([P, H], U32, name="w1_codes", align_bytes=ALIGN)
         w1_scale = keep.tile([P, H], U8, name="w1_scale", align_bytes=ALIGN)
         nc.vector.quantize_mx(out=w1_codes[:].bitcast(FP8X4), scales=w1_scale[:], in_=w1_grouped[:])
@@ -85,10 +90,9 @@ def tile_picked_zmae_mlprelu_po_kernel(
             entries = offsets[:, a * HALF // 16 : (a + 1) * HALF // 16]
             nc.vector.tensor_copy(x_codes[:, a * HALF : (a + 1) * HALF], word_table[:].bitcast(U32).indirect(entries))
 
-        w2_grouped = keep.tile([P, PACK * N], BF16, name="w2_grouped", align_bytes=ALIGN)
-        deal_weights(nc.scalar.copy, w2_grouped, w2_first, W2_SPLIT, P, 0, 2)
-        deal_weights(nc.vector.tensor_copy, w2_grouped, w2_first, 0, W2_SPLIT, 0, 2)
-        deal_weights(nc.vector.tensor_copy, w2_grouped, w2_second, 0, P, 2, PACK)
+        w2_grouped = keep.tile([P, PACK * N], BF16, name="w2_grouped", tag="word_table", align_bytes=ALIGN)
+        deal_weights(nc.vector.tensor_copy, w2_grouped, 0, P // 2, w2_first, 0)
+        deal_weights(nc.vector.tensor_copy, w2_grouped, P // 2, P, w2_second, P // 2)
 
         windows = []
         for t in range(PACK):
@@ -135,9 +139,10 @@ def tile_picked_zmae_mlprelu_po_kernel(
             )
 
         quantize_h(0)
-        quantize_w2(0, N // 2)
-        quantize_h(1)
+        quantize_w2(0, P)
+        quantize_w2(P, N // 2)
         quantize_w2(N // 2, N)
+        quantize_h(1)
 
         ys = []
         for t in range(PACK):
@@ -159,11 +164,11 @@ def tile_picked_zmae_mlprelu_po_kernel(
             ys.append(y)
 
         pairs = [
-            keep.tile([P, 2, CHUNK, 2], BF16, name=f"pairs{c}", align_bytes=ALIGN) for c in range(N_CHUNKS)
+            keep.tile([P, 2, WIDTHS[c], 2], BF16, name=f"pairs{c}", align_bytes=ALIGN) for c in range(N_CHUNKS)
         ]
 
         def round_plane(copy, t, c):
-            copy(out=pairs[c][:, t // 2, :, t % 2], in_=windows[t][:, c * CHUNK : (c + 1) * CHUNK])
+            copy(out=pairs[c][:, t // 2, :, t % 2], in_=windows[t][:, STARTS[c] : STARTS[c] + WIDTHS[c]])
 
         for t in range(PACK):
             width = HALF if t == 0 else S
@@ -171,16 +176,17 @@ def tile_picked_zmae_mlprelu_po_kernel(
                 entries = offsets[:, c0 // 16 : (c0 + width) // 16]
                 nc.vector.tensor_copy(windows[t][:].indirect(entries), ys[t][:, c0 : c0 + width])
             nc.sync.dma_start(out_rows[:, t, :], windows[t][:])
-            for c in range(0 if t < 2 else 1, N_CHUNKS):
+            for c in range(0 if t < 2 else VECTOR_ROUNDS, N_CHUNKS):
                 round_plane(nc.scalar.copy, t, c)
 
         out_scale = keep.tile([P, T // QUADS], U8, name="out_scale", align_bytes=ALIGN)
         grouped = [
-            keep.tile([P, CHUNK * PACK], BF16, name=f"grouped{c}", align_bytes=ALIGN) for c in range(N_CHUNKS)
+            keep.tile([P, WIDTHS[c] * PACK], BF16, name=f"grouped{c}", align_bytes=ALIGN) for c in range(N_CHUNKS)
         ]
-        store_width = STORE_CHUNKS * CHUNK
+        store_starts = [0] + STORE_ENDS[:-1]
         codes = [
-            keep.tile([P, store_width], I32, name=f"codes{s}", align_bytes=ALIGN) for s in range(T // store_width)
+            keep.tile([P, end - start], I32, name=f"codes{start}", align_bytes=ALIGN)
+            for start, end in zip(store_starts, STORE_ENDS)
         ]
 
         def weave(copy, c):
@@ -190,20 +196,24 @@ def tile_picked_zmae_mlprelu_po_kernel(
             )
 
         def quantize_out(c):
-            s, r = divmod(c, STORE_CHUNKS)
+            start, end = STARTS[c], STARTS[c] + WIDTHS[c]
+            store = max(i for i, first in enumerate(store_starts) if first <= start)
+            first = store_starts[store]
+            s, r = divmod(start, QUARTER)
             nc.vector.quantize_mx(
-                out=codes[s][:, r * CHUNK : (r + 1) * CHUNK].bitcast(FP8X4),
-                scales=out_scale[4 * s :, r * CHUNK : (r + 1) * CHUNK],
+                out=codes[store][:, start - first : end - first].bitcast(FP8X4),
+                scales=out_scale[4 * s :, r : r + WIDTHS[c]],
                 in_=grouped[c][:],
             )
-            if r == STORE_CHUNKS - 1:
-                nc.sync.dma_start(out_words[:, s * store_width : (s + 1) * store_width], codes[s][:])
+            if end == STORE_ENDS[store]:
+                nc.sync.dma_start(out_words[:, first:end], codes[store][:])
 
         vector_weaves = N_CHUNKS - SCALAR_WEAVES
         for c in range(vector_weaves, N_CHUNKS):
             weave(nc.scalar.copy, c)
-        round_plane(nc.vector.tensor_copy, 3, 0)
-        round_plane(nc.vector.tensor_copy, 2, 0)
+        for t in (2, 3):
+            for c in range(VECTOR_ROUNDS):
+                round_plane(nc.vector.tensor_copy, t, c)
         for step in range(N_CHUNKS + 1):
             if step < vector_weaves:
                 weave(nc.vector.tensor_copy, step)
@@ -211,8 +221,7 @@ def tile_picked_zmae_mlprelu_po_kernel(
                 quantize_out(step - 1)
 
         for q in range(QUADS):
-            queue = nc.sync if q == QUADS - 1 else nc.scalar
-            queue.dma_start(
+            nc.sync.dma_start(
                 out_2[0, 4 * q : 4 * q + 4, :].bitcast(I32).rearrange("r (s c) -> s r c", s=QUADS),
                 out_scale[32 * q : 32 * q + 16, :].bitcast(I32),
             )

@@ -13,6 +13,8 @@ U16 = mybir.dt.uint16
 U8 = mybir.dt.uint8
 FP8X4 = mybir.dt.float8_e4m3fn_x4
 RELU = mybir.ActivationFunctionType.Relu
+MULT = mybir.AluOpType.mult
+ADD = mybir.AluOpType.add
 
 P = 128
 PACK = 4
@@ -22,13 +24,11 @@ HALF = S // 2
 N1 = 128
 CHUNK = 256
 EDGE = CHUNK // 2
-WIDTHS = [EDGE, EDGE] + [CHUNK] * (T // CHUNK - 2) + [EDGE, EDGE]
-STARTS = [sum(WIDTHS[:c]) for c in range(len(WIDTHS))]
-N_CHUNKS = len(WIDTHS)
-VECTOR_ROUNDS = 2
-SCALAR_WEAVES = 3
 QUARTER = T // QUADS
-STORE_ENDS = [QUARTER, 2 * QUARTER, 3 * QUARTER, T - CHUNK, T]
+MIDDLE = T // 2
+VECTOR_PIECES = [(0, 128), (128, 256), (256, 512), (512, 768), (768, 896)]
+SCALAR_PIECES = [(1024, 1280), (1280, 1536), (1536, 1792), (1792, 2048), (896, 1024)]
+STORES = [(0, 512), (1024, 1536), (512, 768), (1536, 2048), (768, 1024)]
 W1_SPLIT = 80
 
 
@@ -163,12 +163,27 @@ def tile_picked_zmae_mlprelu_po_kernel(
                 nc.scalar.copy(out=y[:, cols], in_=bank[:])
             ys.append(y)
 
-        pairs = [
-            keep.tile([P, 2, WIDTHS[c], 2], BF16, name=f"pairs{c}", align_bytes=ALIGN) for c in range(N_CHUNKS)
+        grouped = [
+            keep.tile([P, QUARTER * PACK], BF16, name=f"grouped{s}", align_bytes=ALIGN) for s in range(QUADS)
         ]
 
-        def round_plane(copy, t, c):
-            copy(out=pairs[c][:, t // 2, :, t % 2], in_=windows[t][:, STARTS[c] : STARTS[c] + WIDTHS[c]])
+        def slots(c0, c1):
+            s, r = divmod(c0, QUARTER)
+            return grouped[s][:, r * PACK : (r + c1 - c0) * PACK].rearrange("p (c t) -> p c t", t=PACK)
+
+        def place(copy, t, c0, c1):
+            copy(out=slots(c0, c1)[:, :, t], in_=windows[t][:, c0:c1])
+
+        def place_gpsimd(t, c0, c1):
+            reach = 2 if t == 2 else 1
+            nc.gpsimd.tensor_scalar(
+                slots(c0, c1)[:, :, t : t + reach],
+                windows[t][:, c0:c1].unsqueeze(2).to_broadcast([P, c1 - c0, reach]),
+                1.0,
+                0.0,
+                MULT,
+                ADD,
+            )
 
         for t in range(PACK):
             width = HALF if t == 0 else S
@@ -176,49 +191,40 @@ def tile_picked_zmae_mlprelu_po_kernel(
                 entries = offsets[:, c0 // 16 : (c0 + width) // 16]
                 nc.vector.tensor_copy(windows[t][:].indirect(entries), ys[t][:, c0 : c0 + width])
             nc.sync.dma_start(out_rows[:, t, :], windows[t][:])
-            for c in range(0 if t < 2 else VECTOR_ROUNDS, N_CHUNKS):
-                round_plane(nc.scalar.copy, t, c)
+            if t < PACK - 1:
+                for c0 in range(0, MIDDLE, QUARTER):
+                    place_gpsimd(t, c0, c0 + QUARTER)
+                    place(nc.scalar.copy, t, MIDDLE + c0, MIDDLE + c0 + QUARTER)
 
         out_scale = keep.tile([P, T // QUADS], U8, name="out_scale", align_bytes=ALIGN)
-        grouped = [
-            keep.tile([P, WIDTHS[c] * PACK], BF16, name=f"grouped{c}", align_bytes=ALIGN) for c in range(N_CHUNKS)
-        ]
-        store_starts = [0] + STORE_ENDS[:-1]
         codes = [
-            keep.tile([P, end - start], I32, name=f"codes{start}", align_bytes=ALIGN)
-            for start, end in zip(store_starts, STORE_ENDS)
+            keep.tile([P, end - start], I32, name=f"codes{start}", align_bytes=ALIGN) for start, end in STORES
         ]
+        done = []
 
-        def weave(copy, c):
-            copy(
-                out=grouped[c][:].bitcast(F32).rearrange("p (c u) -> p c u", u=2),
-                in_=pairs[c][:].rearrange("p u c e -> p u (c e)").bitcast(F32).rearrange("p u c -> p c u"),
-            )
-
-        def quantize_out(c):
-            start, end = STARTS[c], STARTS[c] + WIDTHS[c]
-            store = max(i for i, first in enumerate(store_starts) if first <= start)
-            first = store_starts[store]
-            s, r = divmod(start, QUARTER)
+        def quantize_out(c0, c1):
+            store = [i for i, (start, end) in enumerate(STORES) if start <= c0 < end][0]
+            start, end = STORES[store]
+            s, r = divmod(c0, QUARTER)
             nc.vector.quantize_mx(
-                out=codes[store][:, start - first : end - first].bitcast(FP8X4),
-                scales=out_scale[4 * s :, r : r + WIDTHS[c]],
-                in_=grouped[c][:],
+                out=codes[store][:, c0 - start : c1 - start].bitcast(FP8X4),
+                scales=out_scale[4 * s :, r : r + c1 - c0],
+                in_=grouped[s][:, r * PACK : (r + c1 - c0) * PACK],
             )
-            if end == STORE_ENDS[store]:
-                nc.sync.dma_start(out_words[:, first:end], codes[store][:])
+            done.append((c0, c1))
+            if sum(b - a for a, b in done if start <= a < end) == end - start:
+                nc.sync.dma_start(out_words[:, start:end], codes[store][:])
 
-        vector_weaves = N_CHUNKS - SCALAR_WEAVES
-        for c in range(vector_weaves, N_CHUNKS):
-            weave(nc.scalar.copy, c)
-        for t in (2, 3):
-            for c in range(VECTOR_ROUNDS):
-                round_plane(nc.vector.tensor_copy, t, c)
-        for step in range(N_CHUNKS + 1):
-            if step < vector_weaves:
-                weave(nc.vector.tensor_copy, step)
-            if step >= 1:
-                quantize_out(step - 1)
+        for c0, c1 in SCALAR_PIECES:
+            place(nc.scalar.copy, PACK - 1, c0, c1)
+        place(nc.vector.tensor_copy, PACK - 1, *VECTOR_PIECES[0])
+        for step in range(1, len(VECTOR_PIECES) + 1):
+            if step < len(VECTOR_PIECES):
+                place(nc.vector.tensor_copy, PACK - 1, *VECTOR_PIECES[step])
+            quantize_out(*VECTOR_PIECES[step - 1])
+            if step >= 2:
+                quantize_out(*SCALAR_PIECES[step - 2])
+        quantize_out(*SCALAR_PIECES[-1])
 
         for q in range(QUADS):
             nc.sync.dma_start(

@@ -52,7 +52,6 @@ def tile_picked_zmae_mlprelu_po_kernel(
         psum = ctx.enter_context(tc.psum_pool(name="psum", bufs=8))
 
         offsets = keep.tile([P, S // 16], U16, name="offsets")
-        nc.sync.dma_start(offsets[:], offs)
 
         scale_rows = keep.tile([P, T], U8, name="scale_rows", align_bytes=ALIGN)
         scale_table = keep.tile([P, T], U8, name="scale_table", align_bytes=ALIGN)
@@ -62,6 +61,8 @@ def tile_picked_zmae_mlprelu_po_kernel(
             queue = nc.sync if q < 2 else nc.scalar
             queue.dma_start(scale_rows[rows, :].bitcast(I32), x_scales[0, 4 * q : 4 * q + 4, :].bitcast(I32))
             nc.vector.tensor_copy(scale_table[rows, :].bitcast(I32), scale_rows[rows, :].bitcast(I32))
+
+        nc.sync.dma_start(offsets[:], offs)
 
         w1_raw = keep.tile([P, PACK * H], F32, name="w1_raw", align_bytes=ALIGN)
         nc.sync.dma_start(w1_raw[:], w1.rearrange("(p j) c -> p (j c)", j=PACK))
@@ -127,9 +128,13 @@ def tile_picked_zmae_mlprelu_po_kernel(
         w2_codes = keep.tile([P, N], U32, name="w2_codes", align_bytes=ALIGN)
         w2_scale = keep.tile([P, N], U8, name="w2_scale", align_bytes=ALIGN)
 
-        def quantize_h(a):
-            cols = slice(a * HALF, (a + 1) * HALF)
-            nc.vector.quantize_mx(out=h_codes[:, cols].bitcast(FP8X4), scales=h_scale[:, cols], in_=h_grouped[a][:])
+        def quantize_h(c0, c1):
+            a, r = divmod(c0, HALF)
+            nc.vector.quantize_mx(
+                out=h_codes[:, c0:c1].bitcast(FP8X4),
+                scales=h_scale[:, c0:c1],
+                in_=h_grouped[a][:, r * PACK : (r + c1 - c0) * PACK],
+            )
 
         def quantize_w2(c0, c1):
             nc.vector.quantize_mx(
@@ -138,19 +143,20 @@ def tile_picked_zmae_mlprelu_po_kernel(
                 in_=w2_grouped[:, c0 * PACK : c1 * PACK],
             )
 
-        quantize_h(0)
+        quantize_h(0, HALF)
         quantize_w2(0, P)
+        quantize_h(HALF, S - N1)
+        quantize_h(S - N1, S)
         quantize_w2(P, N // 2)
         quantize_w2(N // 2, N)
-        quantize_h(1)
 
         ys = []
         for t in range(PACK):
             y = keep.tile([P, S], F32, name=f"y{t}", align_bytes=ALIGN)
-            width = HALF if t == 0 else S
-            for c0 in range(0, S, width):
-                cols = slice(c0, c0 + width)
-                bank = psum.tile([P, width], F32, name="bank", tag="bank")
+            ends = [HALF, S - N1, S] if t == 0 else [S]
+            for c0, c1 in zip([0] + ends, ends):
+                cols = slice(c0, c1)
+                bank = psum.tile([P, c1 - c0], F32, name="bank", tag="bank")
                 nc.tensor.matmul_mx(
                     out=bank[:],
                     lhsT=w2_codes[:, t * P : (t + 1) * P].bitcast(FP8X4),
@@ -186,10 +192,7 @@ def tile_picked_zmae_mlprelu_po_kernel(
             )
 
         for t in range(PACK):
-            width = HALF if t == 0 else S
-            for c0 in range(0, S, width):
-                entries = offsets[:, c0 // 16 : (c0 + width) // 16]
-                nc.vector.tensor_copy(windows[t][:].indirect(entries), ys[t][:, c0 : c0 + width])
+            nc.vector.tensor_copy(windows[t][:].indirect(offsets[:]), ys[t][:])
             nc.sync.dma_start(out_rows[:, t, :], windows[t][:])
             if t < PACK - 1:
                 for c0 in range(0, MIDDLE, QUARTER):

@@ -28,7 +28,7 @@ QUARTER = T // QUADS
 MIDDLE = T // 2
 VECTOR_PIECES = [(0, 128), (128, 256), (256, 512), (512, 768), (768, 896)]
 SCALAR_PIECES = [(1024, 1280), (1280, 1536), (1536, 1792), (1792, 2048), (896, 1024)]
-STORES = [(0, 512), (1024, 1536), (512, 768), (1536, 2048), (768, 1024)]
+STORES = [(0, 512), (512, 768), (768, 1024)]
 W1_SPLIT = 80
 
 
@@ -45,7 +45,7 @@ def tile_picked_zmae_mlprelu_po_kernel(
     nc = tc.nc
     mask_rows = mask.rearrange("(p t) c -> p t c", t=PACK)
     out_rows = out_0.rearrange("(p t) c -> p t c", t=PACK)
-    out_words = out_1[0].rearrange("p c r -> p (c r)").bitcast(I32)
+    out_words = out_1[0].rearrange("p c r -> p (c r)").bitcast(I32).rearrange("p (h c) -> p h c", h=2)
 
     with ExitStack() as ctx:
         keep = ctx.enter_context(tc.tile_pool(name="keep", bufs=1))
@@ -201,22 +201,26 @@ def tile_picked_zmae_mlprelu_po_kernel(
 
         out_scale = keep.tile([P, T // QUADS], U8, name="out_scale", align_bytes=ALIGN)
         codes = [
-            keep.tile([P, end - start], I32, name=f"codes{start}", align_bytes=ALIGN) for start, end in STORES
+            keep.tile([P, 2 * (end - start)], I32, name=f"codes{start}", align_bytes=ALIGN) for start, end in STORES
         ]
         done = []
 
         def quantize_out(c0, c1):
-            store = [i for i, (start, end) in enumerate(STORES) if start <= c0 < end][0]
+            half, col = divmod(c0, MIDDLE)
+            store = [i for i, (start, end) in enumerate(STORES) if start <= col < end][0]
             start, end = STORES[store]
+            first = half * (end - start) + col - start
             s, r = divmod(c0, QUARTER)
             nc.vector.quantize_mx(
-                out=codes[store][:, c0 - start : c1 - start].bitcast(FP8X4),
+                out=codes[store][:, first : first + c1 - c0].bitcast(FP8X4),
                 scales=out_scale[4 * s :, r : r + c1 - c0],
                 in_=grouped[s][:, r * PACK : (r + c1 - c0) * PACK],
             )
             done.append((c0, c1))
-            if sum(b - a for a, b in done if start <= a < end) == end - start:
-                nc.sync.dma_start(out_words[:, start:end], codes[store][:])
+            if sum(b - a for a, b in done if start <= a % MIDDLE < end) == 2 * (end - start):
+                nc.sync.dma_start(
+                    out_words[:, :, start:end], codes[store][:].rearrange("p (h c) -> p h c", h=2)
+                )
 
         for c0, c1 in SCALAR_PIECES:
             place(nc.scalar.copy, PACK - 1, c0, c1)

@@ -19,23 +19,28 @@ ADD = mybir.AluOpType.add
 P = 128
 PACK = 4
 QUADS = 4
+PSUM_BANKS = 8
 ALIGN = 64
+PER_COLUMN = 16
 HALF = S // 2
-N1 = 128
-CHUNK = 256
-EDGE = CHUNK // 2
+BANK_ENTRIES = 128
+W1_VECTOR_GROUPS = 80
+
 QUARTER = T // QUADS
 MIDDLE = T // 2
-VECTOR_PIECES = [(0, 128), (128, 256), (256, 512), (512, 768), (768, 896)]
-SCALAR_PIECES = [(1024, 1280), (1280, 1536), (1536, 1792), (1792, 2048), (896, 1024)]
-STORES = [(0, 512), (512, 768), (768, 1024)]
-W1_SPLIT = 80
+CHUNK = 256
+SHORT = CHUNK // 2
+VECTOR_CUTS = [0, SHORT] + list(range(CHUNK, MIDDLE, CHUNK)) + [MIDDLE - SHORT]
+VECTOR_PIECES = list(zip(VECTOR_CUTS, VECTOR_CUTS[1:]))
+SCALAR_PIECES = [(c, c + CHUNK) for c in range(MIDDLE, T, CHUNK)] + [(MIDDLE - SHORT, MIDDLE)]
+STORE_CUTS = [0, 2 * CHUNK, 3 * CHUNK, MIDDLE]
+STORE_SPANS = list(zip(STORE_CUTS, STORE_CUTS[1:]))
 
 
-def deal_weights(copy, grouped, m0, m1, raw, first):
+def deal_weights(copy, grouped, m0, m1, raw, raw_m0):
     copy(
         out=grouped[:].rearrange("p (t m j) -> p m j t", t=PACK, j=PACK)[:, m0:m1],
-        in_=raw[:].rearrange("p (j m t) -> p m j t", j=PACK, t=PACK)[:, m0 - first : m1 - first],
+        in_=raw[:].rearrange("p (j m t) -> p m j t", j=PACK, t=PACK)[:, m0 - raw_m0 : m1 - raw_m0],
     )
 
 
@@ -43,22 +48,22 @@ def tile_picked_zmae_mlprelu_po_kernel(
     tc, x_words, x_scales, mask, w1, w2, offs, out_0, out_1, out_2
 ):
     nc = tc.nc
-    mask_rows = mask.rearrange("(p t) c -> p t c", t=PACK)
-    out_rows = out_0.rearrange("(p t) c -> p t c", t=PACK)
-    out_words = out_1[0].rearrange("p c r -> p (c r)").bitcast(I32).rearrange("p (h c) -> p h c", h=2)
+    mask_planes = mask.rearrange("(p t) c -> p t c", t=PACK)
+    out_planes = out_0.rearrange("(p t) c -> p t c", t=PACK)
+    out_words = out_1[0].rearrange("p c r -> p (c r)").bitcast(I32).rearrange("p (side c) -> p side c", side=2)
 
     with ExitStack() as ctx:
         keep = ctx.enter_context(tc.tile_pool(name="keep", bufs=1))
-        psum = ctx.enter_context(tc.psum_pool(name="psum", bufs=8))
+        psum = ctx.enter_context(tc.psum_pool(name="psum", bufs=PSUM_BANKS))
 
-        offsets = keep.tile([P, S // 16], U16, name="offsets")
+        offsets = keep.tile([P, S // PER_COLUMN], U16, name="offsets")
 
         scale_rows = keep.tile([P, T], U8, name="scale_rows", align_bytes=ALIGN)
         scale_table = keep.tile([P, T], U8, name="scale_table", align_bytes=ALIGN)
         nc.vector.memset(scale_table[:].bitcast(I32), 0)
         for q in range(QUADS):
             rows = slice(32 * q, 32 * q + 4)
-            queue = nc.sync if q < 2 else nc.scalar
+            queue = nc.sync if q < QUADS // 2 else nc.scalar
             queue.dma_start(scale_rows[rows, :].bitcast(I32), x_scales[0, 4 * q : 4 * q + 4, :].bitcast(I32))
             nc.vector.tensor_copy(scale_table[rows, :].bitcast(I32), scale_rows[rows, :].bitcast(I32))
 
@@ -71,54 +76,54 @@ def tile_picked_zmae_mlprelu_po_kernel(
         nc.sync.dma_start(word_table[:], x_words[0].rearrange("p c r -> p (c r)").bitcast(I32))
 
         w2_rows = w2.rearrange("(p j) c -> p j c", j=PACK)
-        w2_first = keep.tile([P, 2 * N], F32, name="w2_first", align_bytes=ALIGN)
-        nc.sync.dma_start(w2_first[:].rearrange("p (j c) -> p j c", j=PACK), w2_rows[:, :, : N // 2])
-        w2_second = keep.tile([P, 2 * N], F32, name="w2_second", align_bytes=ALIGN)
-        nc.sync.dma_start(w2_second[:].rearrange("p (j c) -> p j c", j=PACK), w2_rows[:, :, N // 2 :])
+        w2_left = keep.tile([P, PACK * N // 2], F32, name="w2_left", align_bytes=ALIGN)
+        nc.sync.dma_start(w2_left[:].rearrange("p (j c) -> p j c", j=PACK), w2_rows[:, :, : N // 2])
+        w2_right = keep.tile([P, PACK * N // 2], F32, name="w2_right", align_bytes=ALIGN)
+        nc.sync.dma_start(w2_right[:].rearrange("p (j c) -> p j c", j=PACK), w2_rows[:, :, N // 2 :])
 
         x_scale = keep.tile([P, S], U8, name="x_scale", align_bytes=ALIGN)
         nc.vector.tensor_copy(x_scale[:], scale_table[:].indirect(offsets[:]))
 
         w1_grouped = keep.tile([P, PACK * H], BF16, name="w1_grouped", tag="x_codes", align_bytes=ALIGN)
-        deal_weights(nc.vector.tensor_copy, w1_grouped, 0, W1_SPLIT, w1_raw, 0)
-        deal_weights(nc.scalar.copy, w1_grouped, W1_SPLIT, P, w1_raw, 0)
+        deal_weights(nc.vector.tensor_copy, w1_grouped, 0, W1_VECTOR_GROUPS, w1_raw, 0)
+        deal_weights(nc.scalar.copy, w1_grouped, W1_VECTOR_GROUPS, P, w1_raw, 0)
         w1_codes = keep.tile([P, H], U32, name="w1_codes", align_bytes=ALIGN)
         w1_scale = keep.tile([P, H], U8, name="w1_scale", align_bytes=ALIGN)
         nc.vector.quantize_mx(out=w1_codes[:].bitcast(FP8X4), scales=w1_scale[:], in_=w1_grouped[:])
 
         x_codes = keep.tile([P, S], U32, name="x_codes", tag="x_codes", align_bytes=ALIGN)
-        for a in range(2):
-            entries = offsets[:, a * HALF // 16 : (a + 1) * HALF // 16]
-            nc.vector.tensor_copy(x_codes[:, a * HALF : (a + 1) * HALF], word_table[:].bitcast(U32).indirect(entries))
+        for j0 in range(0, S, HALF):
+            entries = offsets[:, j0 // PER_COLUMN : (j0 + HALF) // PER_COLUMN]
+            nc.vector.tensor_copy(x_codes[:, j0 : j0 + HALF], word_table[:].bitcast(U32).indirect(entries))
 
         w2_grouped = keep.tile([P, PACK * N], BF16, name="w2_grouped", tag="word_table", align_bytes=ALIGN)
-        deal_weights(nc.vector.tensor_copy, w2_grouped, 0, P // 2, w2_first, 0)
-        deal_weights(nc.vector.tensor_copy, w2_grouped, P // 2, P, w2_second, P // 2)
+        deal_weights(nc.vector.tensor_copy, w2_grouped, 0, P // 2, w2_left, 0)
+        deal_weights(nc.vector.tensor_copy, w2_grouped, P // 2, P, w2_right, P // 2)
 
         windows = []
         for t in range(PACK):
             window = keep.tile([P, T], F32, name=f"window{t}", align_bytes=ALIGN)
-            nc.sync.dma_start(window[:], mask_rows[:, t, :])
+            nc.sync.dma_start(window[:], mask_planes[:, t, :])
             windows.append(window)
 
         h_grouped = [
-            keep.tile([P, HALF * PACK], BF16, name=f"h_grouped{a}", align_bytes=ALIGN) for a in range(2)
+            keep.tile([P, HALF * PACK], BF16, name=f"h_grouped{half}", align_bytes=ALIGN) for half in range(2)
         ]
-        for c in range(S // N1):
-            a, c0 = divmod(c * N1, HALF)
-            bank = psum.tile([P, PACK, N1], F32, name="bank", tag="bank")
+        for j0 in range(0, S, BANK_ENTRIES):
+            half, r = divmod(j0, HALF)
+            bank = psum.tile([P, PACK, BANK_ENTRIES], F32, name="bank", tag="bank")
             for t in range(PACK):
                 nc.tensor.matmul_mx(
                     out=bank[:, t, :],
                     lhsT=w1_codes[:, t * P : (t + 1) * P].bitcast(FP8X4),
                     lhsT_scale=w1_scale[:, t * P : (t + 1) * P],
-                    rhs=x_codes[:, c * N1 : (c + 1) * N1].bitcast(FP8X4),
-                    rhs_scale=x_scale[:, c * N1 : (c + 1) * N1],
+                    rhs=x_codes[:, j0 : j0 + BANK_ENTRIES].bitcast(FP8X4),
+                    rhs_scale=x_scale[:, j0 : j0 + BANK_ENTRIES],
                     start=True,
                     stop=True,
                 )
             nc.scalar.activation(
-                out=h_grouped[a][:, c0 * PACK : (c0 + N1) * PACK].rearrange("p (n t) -> p n t", t=PACK),
+                out=h_grouped[half][:, r * PACK : (r + BANK_ENTRIES) * PACK].rearrange("p (n t) -> p n t", t=PACK),
                 in_=bank[:].rearrange("p t n -> p n t"),
                 func=RELU,
             )
@@ -128,110 +133,113 @@ def tile_picked_zmae_mlprelu_po_kernel(
         w2_codes = keep.tile([P, N], U32, name="w2_codes", align_bytes=ALIGN)
         w2_scale = keep.tile([P, N], U8, name="w2_scale", align_bytes=ALIGN)
 
-        def quantize_h(c0, c1):
-            a, r = divmod(c0, HALF)
+        def quantize_h(j0, j1):
+            half, r = divmod(j0, HALF)
             nc.vector.quantize_mx(
-                out=h_codes[:, c0:c1].bitcast(FP8X4),
-                scales=h_scale[:, c0:c1],
-                in_=h_grouped[a][:, r * PACK : (r + c1 - c0) * PACK],
+                out=h_codes[:, j0:j1].bitcast(FP8X4),
+                scales=h_scale[:, j0:j1],
+                in_=h_grouped[half][:, r * PACK : (r + j1 - j0) * PACK],
             )
 
-        def quantize_w2(c0, c1):
+        def quantize_w2(m0, m1):
             nc.vector.quantize_mx(
-                out=w2_codes[:, c0:c1].bitcast(FP8X4),
-                scales=w2_scale[:, c0:c1],
-                in_=w2_grouped[:, c0 * PACK : c1 * PACK],
+                out=w2_codes[:, m0:m1].bitcast(FP8X4),
+                scales=w2_scale[:, m0:m1],
+                in_=w2_grouped[:, m0 * PACK : m1 * PACK],
             )
 
+        last_bank = S - BANK_ENTRIES
         quantize_h(0, HALF)
         quantize_w2(0, P)
-        quantize_h(HALF, S - N1)
-        quantize_h(S - N1, S)
-        quantize_w2(P, N // 2)
-        quantize_w2(N // 2, N)
+        quantize_h(HALF, last_bank)
+        quantize_h(last_bank, S)
+        quantize_w2(P, 2 * P)
+        quantize_w2(2 * P, N)
 
-        ys = []
+        y_planes = []
         for t in range(PACK):
             y = keep.tile([P, S], F32, name=f"y{t}", align_bytes=ALIGN)
-            ends = [HALF, S - N1, S] if t == 0 else [S]
-            for c0, c1 in zip([0] + ends, ends):
-                cols = slice(c0, c1)
-                bank = psum.tile([P, c1 - c0], F32, name="bank", tag="bank")
+            cuts = [0, HALF, last_bank, S] if t == 0 else [0, S]
+            for j0, j1 in zip(cuts, cuts[1:]):
+                bank = psum.tile([P, j1 - j0], F32, name="bank", tag="bank")
                 nc.tensor.matmul_mx(
                     out=bank[:],
                     lhsT=w2_codes[:, t * P : (t + 1) * P].bitcast(FP8X4),
                     lhsT_scale=w2_scale[:, t * P : (t + 1) * P],
-                    rhs=h_codes[:, cols].bitcast(FP8X4),
-                    rhs_scale=h_scale[:, cols],
+                    rhs=h_codes[:, j0:j1].bitcast(FP8X4),
+                    rhs_scale=h_scale[:, j0:j1],
                     start=True,
                     stop=True,
                 )
-                nc.scalar.copy(out=y[:, cols], in_=bank[:])
-            ys.append(y)
+                nc.scalar.copy(out=y[:, j0:j1], in_=bank[:])
+            y_planes.append(y)
 
-        grouped = [
-            keep.tile([P, QUARTER * PACK], BF16, name=f"grouped{s}", align_bytes=ALIGN) for s in range(QUADS)
+        out_grouped = [
+            keep.tile([P, QUARTER * PACK], BF16, name=f"out_grouped{s}", align_bytes=ALIGN) for s in range(QUADS)
         ]
 
-        def slots(c0, c1):
+        def grouped_columns(c0, c1):
             s, r = divmod(c0, QUARTER)
-            return grouped[s][:, r * PACK : (r + c1 - c0) * PACK].rearrange("p (c t) -> p c t", t=PACK)
+            return out_grouped[s][:, r * PACK : (r + c1 - c0) * PACK]
 
-        def place(copy, t, c0, c1):
-            copy(out=slots(c0, c1)[:, :, t], in_=windows[t][:, c0:c1])
+        def round_plane(copy, t, c0, c1):
+            places = grouped_columns(c0, c1).rearrange("p (c t) -> p c t", t=PACK)
+            copy(out=places[:, :, t], in_=windows[t][:, c0:c1])
 
-        def place_gpsimd(t, c0, c1):
-            reach = 2 if t == 2 else 1
+        def round_plane_gpsimd(t, c0, c1):
+            reach = 2 if t == PACK - 2 else 1
+            places = grouped_columns(c0, c1).rearrange("p (c t) -> p c t", t=PACK)
             nc.gpsimd.tensor_scalar(
-                slots(c0, c1)[:, :, t : t + reach],
+                places[:, :, t : t + reach],
                 windows[t][:, c0:c1].unsqueeze(2).to_broadcast([P, c1 - c0, reach]),
                 1.0,
-                0.0,
+                -0.0,
                 MULT,
                 ADD,
             )
 
         for t in range(PACK):
-            nc.vector.tensor_copy(windows[t][:].indirect(offsets[:]), ys[t][:])
-            nc.sync.dma_start(out_rows[:, t, :], windows[t][:])
+            nc.vector.tensor_copy(windows[t][:].indirect(offsets[:]), y_planes[t][:])
+            nc.sync.dma_start(out_planes[:, t, :], windows[t][:])
             if t < PACK - 1:
                 for c0 in range(0, MIDDLE, QUARTER):
-                    place_gpsimd(t, c0, c0 + QUARTER)
-                    place(nc.scalar.copy, t, MIDDLE + c0, MIDDLE + c0 + QUARTER)
+                    round_plane_gpsimd(t, c0, c0 + QUARTER)
+                    round_plane(nc.scalar.copy, t, MIDDLE + c0, MIDDLE + c0 + QUARTER)
 
-        out_scale = keep.tile([P, T // QUADS], U8, name="out_scale", align_bytes=ALIGN)
-        codes = [
-            keep.tile([P, 2 * (end - start)], I32, name=f"codes{start}", align_bytes=ALIGN) for start, end in STORES
+        out_scale = keep.tile([P, QUARTER], U8, name="out_scale", align_bytes=ALIGN)
+        out_codes = [
+            keep.tile([P, 2 * (end - start)], I32, name=f"out_codes{start}", align_bytes=ALIGN)
+            for start, end in STORE_SPANS
         ]
-        done = []
+        quantized = []
 
         def quantize_out(c0, c1):
-            half, col = divmod(c0, MIDDLE)
-            store = [i for i, (start, end) in enumerate(STORES) if start <= col < end][0]
-            start, end = STORES[store]
-            first = half * (end - start) + col - start
+            side, col = divmod(c0, MIDDLE)
+            store = [i for i, (start, end) in enumerate(STORE_SPANS) if start <= col < end][0]
+            start, end = STORE_SPANS[store]
+            first = side * (end - start) + col - start
             s, r = divmod(c0, QUARTER)
             nc.vector.quantize_mx(
-                out=codes[store][:, first : first + c1 - c0].bitcast(FP8X4),
+                out=out_codes[store][:, first : first + c1 - c0].bitcast(FP8X4),
                 scales=out_scale[4 * s :, r : r + c1 - c0],
-                in_=grouped[s][:, r * PACK : (r + c1 - c0) * PACK],
+                in_=grouped_columns(c0, c1),
             )
-            done.append((c0, c1))
-            if sum(b - a for a, b in done if start <= a % MIDDLE < end) == 2 * (end - start):
+            quantized.append((c0, c1))
+            if sum(b - a for a, b in quantized if start <= a % MIDDLE < end) == 2 * (end - start):
                 nc.sync.dma_start(
-                    out_words[:, :, start:end], codes[store][:].rearrange("p (h c) -> p h c", h=2)
+                    out_words[:, :, start:end], out_codes[store][:].rearrange("p (side c) -> p side c", side=2)
                 )
 
         for c0, c1 in SCALAR_PIECES:
-            place(nc.scalar.copy, PACK - 1, c0, c1)
-        place(nc.vector.tensor_copy, PACK - 1, *VECTOR_PIECES[0])
-        for step in range(1, len(VECTOR_PIECES) + 1):
-            if step < len(VECTOR_PIECES):
-                place(nc.vector.tensor_copy, PACK - 1, *VECTOR_PIECES[step])
-            quantize_out(*VECTOR_PIECES[step - 1])
+            round_plane(nc.scalar.copy, PACK - 1, c0, c1)
+        steps = len(VECTOR_PIECES)
+        for step in range(steps + 2):
+            if step < steps:
+                round_plane(nc.vector.tensor_copy, PACK - 1, *VECTOR_PIECES[step])
+            if 1 <= step <= steps:
+                quantize_out(*VECTOR_PIECES[step - 1])
             if step >= 2:
                 quantize_out(*SCALAR_PIECES[step - 2])
-        quantize_out(*SCALAR_PIECES[-1])
 
         for q in range(QUADS):
             nc.sync.dma_start(

@@ -30,11 +30,11 @@ QUARTER = T // QUADS
 MIDDLE = T // 2
 CHUNK = 256
 SHORT = CHUNK // 2
-VECTOR_CUTS = [0, SHORT] + list(range(CHUNK, MIDDLE, CHUNK)) + [MIDDLE - SHORT]
-VECTOR_PIECES = list(zip(VECTOR_CUTS, VECTOR_CUTS[1:]))
-SCALAR_PIECES = [(c, c + CHUNK) for c in range(MIDDLE, T, CHUNK)] + [(MIDDLE - SHORT, MIDDLE)]
-STORE_CUTS = [0, 2 * CHUNK, 3 * CHUNK, MIDDLE]
-STORE_SPANS = list(zip(STORE_CUTS, STORE_CUTS[1:]))
+GPSIMD_END = 896
+VECTOR_END = 960
+BOTH = 16
+SCALAR_CUTS = [VECTOR_END, 1280, 1536, 1792, 1920, T]
+SCALAR_PIECES = list(zip(SCALAR_CUTS, SCALAR_CUTS[1:]))
 
 
 def deal_weights(copy, grouped, m0, m1, raw, raw_m0):
@@ -50,7 +50,7 @@ def tile_picked_zmae_mlprelu_po_kernel(
     nc = tc.nc
     mask_planes = mask.rearrange("(p t) c -> p t c", t=PACK)
     out_planes = out_0.rearrange("(p t) c -> p t c", t=PACK)
-    out_words = out_1[0].rearrange("p c r -> p (c r)").bitcast(I32).rearrange("p (side c) -> p side c", side=2)
+    out_words = out_1[0].rearrange("p c r -> p (c r)").bitcast(I32)
 
     with ExitStack() as ctx:
         keep = ctx.enter_context(tc.tile_pool(name="keep", bufs=1))
@@ -174,72 +174,59 @@ def tile_picked_zmae_mlprelu_po_kernel(
                 nc.scalar.copy(out=y[:, j0:j1], in_=bank[:])
             y_planes.append(y)
 
-        out_grouped = [
-            keep.tile([P, QUARTER * PACK], BF16, name=f"out_grouped{s}", align_bytes=ALIGN) for s in range(QUADS)
-        ]
-
-        def grouped_columns(c0, c1):
-            s, r = divmod(c0, QUARTER)
-            return out_grouped[s][:, r * PACK : (r + c1 - c0) * PACK]
+        out_grouped = keep.tile([P, T * PACK], BF16, name="out_grouped", align_bytes=ALIGN)
+        places = out_grouped[:].rearrange("p (c t) -> p c t", t=PACK)
 
         def round_plane(copy, t, c0, c1):
-            places = grouped_columns(c0, c1).rearrange("p (c t) -> p c t", t=PACK)
-            copy(out=places[:, :, t], in_=windows[t][:, c0:c1])
+            copy(out=places[:, c0:c1, t], in_=windows[t][:, c0:c1])
 
-        def round_plane_gpsimd(t, c0, c1):
-            reach = 2 if t == PACK - 2 else 1
-            places = grouped_columns(c0, c1).rearrange("p (c t) -> p c t", t=PACK)
-            nc.gpsimd.tensor_scalar(
-                places[:, :, t : t + reach],
-                windows[t][:, c0:c1].unsqueeze(2).to_broadcast([P, c1 - c0, reach]),
-                1.0,
-                -0.0,
-                MULT,
-                ADD,
-            )
+        def gpsimd_copy(out, in_):
+            nc.gpsimd.tensor_scalar(out, in_, 1.0, -0.0, MULT, ADD)
 
         for t in range(PACK):
             nc.vector.tensor_copy(windows[t][:].indirect(offsets[:]), y_planes[t][:])
             nc.sync.dma_start(out_planes[:, t, :], windows[t][:])
             if t < PACK - 1:
-                for c0 in range(0, MIDDLE, QUARTER):
-                    round_plane_gpsimd(t, c0, c0 + QUARTER)
-                    round_plane(nc.scalar.copy, t, MIDDLE + c0, MIDDLE + c0 + QUARTER)
+                round_plane(gpsimd_copy, t, 0, GPSIMD_END if t == PACK - 2 else MIDDLE)
+                round_plane(nc.scalar.copy, t, VECTOR_END if t == PACK - 2 else MIDDLE, T)
 
         out_scale = keep.tile([P, QUARTER], U8, name="out_scale", align_bytes=ALIGN)
-        out_codes = [
-            keep.tile([P, 2 * (end - start)], I32, name=f"out_codes{start}", align_bytes=ALIGN)
-            for start, end in STORE_SPANS
-        ]
-        quantized = []
+        codes_even = keep.tile([P, 2 * QUARTER], I32, name="codes_even", align_bytes=ALIGN)
+        codes_1 = keep.tile([P, QUARTER], I32, name="codes_1", align_bytes=ALIGN)
+        codes_3 = keep.tile([P, QUARTER], I32, name="codes_3", align_bytes=ALIGN)
+        quarter_codes = [codes_even[:, :QUARTER], codes_1[:], codes_even[:, QUARTER:], codes_3[:]]
 
         def quantize_out(c0, c1):
-            side, col = divmod(c0, MIDDLE)
-            store = [i for i, (start, end) in enumerate(STORE_SPANS) if start <= col < end][0]
-            start, end = STORE_SPANS[store]
-            first = side * (end - start) + col - start
             s, r = divmod(c0, QUARTER)
             nc.vector.quantize_mx(
-                out=out_codes[store][:, first : first + c1 - c0].bitcast(FP8X4),
+                out=quarter_codes[s][:, r : r + c1 - c0].bitcast(FP8X4),
                 scales=out_scale[4 * s :, r : r + c1 - c0],
-                in_=grouped_columns(c0, c1),
+                in_=out_grouped[:, c0 * PACK : c1 * PACK],
             )
-            quantized.append((c0, c1))
-            if sum(b - a for a, b in quantized if start <= a % MIDDLE < end) == 2 * (end - start):
-                nc.sync.dma_start(
-                    out_words[:, :, start:end], out_codes[store][:].rearrange("p (side c) -> p side c", side=2)
-                )
 
         for c0, c1 in SCALAR_PIECES:
             round_plane(nc.scalar.copy, PACK - 1, c0, c1)
-        steps = len(VECTOR_PIECES)
-        for step in range(steps + 2):
-            if step < steps:
-                round_plane(nc.vector.tensor_copy, PACK - 1, *VECTOR_PIECES[step])
-            if 1 <= step <= steps:
-                quantize_out(*VECTOR_PIECES[step - 1])
-            if step >= 2:
-                quantize_out(*SCALAR_PIECES[step - 2])
+        vround = nc.vector.tensor_copy
+        c0, c1 = GPSIMD_END - BOTH, VECTOR_END
+        vround(out=places[:, c0:c1, 2:4], in_=windows[3][:, c0:c1].unsqueeze(2).to_broadcast([P, c1 - c0, 2]))
+        round_plane(vround, 3, 0, 256)
+        round_plane(vround, 2, c0, c1)
+        round_plane(vround, 3, 256, 512)
+        quantize_out(0, 256)
+        round_plane(vround, 3, 512, c0)
+        quantize_out(256, 512)
+        quantize_out(1024, 1280)
+        quantize_out(1280, 1536)
+        nc.sync.dma_start(
+            out_words.rearrange("p (side c) -> p side c", side=2)[:, :, :QUARTER],
+            codes_even[:].rearrange("p (side c) -> p side c", side=2),
+        )
+        quantize_out(512, 1024)
+        nc.sync.dma_start(out_words[:, QUARTER:MIDDLE], codes_1[:])
+        quantize_out(1536, 1792)
+        quantize_out(1792, 1920)
+        quantize_out(1920, T)
+        nc.sync.dma_start(out_words[:, MIDDLE + QUARTER :], codes_3[:])
 
         for q in range(QUADS):
             nc.sync.dma_start(

@@ -13,6 +13,7 @@ U16 = mybir.dt.uint16
 U8 = mybir.dt.uint8
 FP8X4 = mybir.dt.float8_e4m3fn_x4
 RELU = mybir.ActivationFunctionType.Relu
+COPY = mybir.ActivationFunctionType.Copy
 MULT = mybir.AluOpType.mult
 ADD = mybir.AluOpType.add
 
@@ -28,13 +29,7 @@ W1_VECTOR_GROUPS = 80
 
 QUARTER = T // QUADS
 MIDDLE = T // 2
-CHUNK = 256
-SHORT = CHUNK // 2
-GPSIMD_END = 896
-VECTOR_END = 960
-BOTH = 16
-SCALAR_CUTS = [VECTOR_END, 1280, 1536, 1792, 1920, T]
-SCALAR_PIECES = list(zip(SCALAR_CUTS, SCALAR_CUTS[1:]))
+LOW = 1280
 
 
 def deal_weights(copy, grouped, m0, m1, raw, raw_m0):
@@ -158,7 +153,7 @@ def tile_picked_zmae_mlprelu_po_kernel(
 
         y_planes = []
         for t in range(PACK):
-            y = keep.tile([P, S], F32, name=f"y{t}", align_bytes=ALIGN)
+            y = keep.tile([P, S], F32, name=f"y{t}", tag=f"y{t}", align_bytes=ALIGN)
             cuts = [0, HALF, last_bank, S] if t == 0 else [0, S]
             for j0, j1 in zip(cuts, cuts[1:]):
                 bank = psum.tile([P, j1 - j0], F32, name="bank", tag="bank")
@@ -174,21 +169,45 @@ def tile_picked_zmae_mlprelu_po_kernel(
                 nc.scalar.copy(out=y[:, j0:j1], in_=bank[:])
             y_planes.append(y)
 
+        low = keep.tile([P, PACK * LOW], BF16, name="low", align_bytes=ALIGN)
         out_grouped = keep.tile([P, T * PACK], BF16, name="out_grouped", align_bytes=ALIGN)
-        places = out_grouped[:].rearrange("p (c t) -> p c t", t=PACK)
-
-        def round_plane(copy, t, c0, c1):
-            copy(out=places[:, c0:c1, t], in_=windows[t][:, c0:c1])
 
         def gpsimd_copy(out, in_):
             nc.gpsimd.tensor_scalar(out, in_, 1.0, -0.0, MULT, ADD)
 
-        for t in range(PACK):
-            nc.vector.tensor_copy(windows[t][:].indirect(offsets[:]), y_planes[t][:])
+        def scatter(t):
+            if t % 2 == 0:
+                nc.vector.tensor_copy(windows[t][:].indirect(offsets[:]), y_planes[t][:])
+            else:
+                for j0 in range(0, S, HALF):
+                    entries = offsets[:, j0 // PER_COLUMN : (j0 + HALF) // PER_COLUMN]
+                    nc.scalar.activation(
+                        out=windows[t][:].indirect(entries), in_=y_planes[t][:, j0 : j0 + HALF], func=COPY
+                    )
             nc.sync.dma_start(out_planes[:, t, :], windows[t][:])
-            if t < PACK - 1:
-                round_plane(gpsimd_copy, t, 0, GPSIMD_END if t == PACK - 2 else MIDDLE)
-                round_plane(nc.scalar.copy, t, VECTOR_END if t == PACK - 2 else MIDDLE, T)
+
+        for t in range(PACK):
+            scatter(t)
+        high = keep.tile([P, PACK * (T - LOW)], BF16, name="high", tag="y2", align_bytes=ALIGN)
+
+        def rounded(c0, c1):
+            tile, base = (low, 0) if c0 < LOW else (high, LOW)
+            return tile[:].rearrange("p (t c) -> p t c", t=PACK)[:, :, c0 - base : c1 - base]
+
+        def round_plane(copy, t, c0, c1):
+            copy(out=rounded(c0, c1)[:, t, :], in_=windows[t][:, c0:c1])
+
+        def group(copy, c0, c1):
+            copy(
+                out=out_grouped[:, c0 * PACK : c1 * PACK].rearrange("p (c i t) -> p c t i", i=PACK, t=PACK),
+                in_=rounded(c0, c1).rearrange("p t (c i) -> p c t i", i=PACK),
+            )
+
+        for t in range(2):
+            round_plane(gpsimd_copy, t, 0, LOW)
+        round_plane(nc.vector.tensor_copy, 2, 0, LOW)
+        for t in range(3):
+            round_plane(nc.vector.tensor_copy, t, LOW, T)
 
         out_scale = keep.tile([P, QUARTER], U8, name="out_scale", align_bytes=ALIGN)
         codes_even = keep.tile([P, 2 * QUARTER], I32, name="codes_even", align_bytes=ALIGN)
@@ -204,18 +223,22 @@ def tile_picked_zmae_mlprelu_po_kernel(
                 in_=out_grouped[:, c0 * PACK : c1 * PACK],
             )
 
-        for c0, c1 in SCALAR_PIECES:
-            round_plane(nc.scalar.copy, PACK - 1, c0, c1)
-        vround = nc.vector.tensor_copy
-        c0, c1 = GPSIMD_END - BOTH, VECTOR_END
-        vround(out=places[:, c0:c1, 2:4], in_=windows[3][:, c0:c1].unsqueeze(2).to_broadcast([P, c1 - c0, 2]))
-        round_plane(vround, 3, 0, 256)
-        round_plane(vround, 2, c0, c1)
-        round_plane(vround, 3, 256, 512)
+        vcopy = nc.vector.tensor_copy
+        scopy = nc.scalar.copy
+        round_plane(scopy, 3, 1024, LOW)
+        round_plane(scopy, 3, LOW, 1536)
+        round_plane(vcopy, 3, 0, 512)
+        round_plane(vcopy, 3, 512, 1024)
+        round_plane(vcopy, 3, 1536, T)
+        for c0, c1 in [(1024, 1280), (1280, 1536), (1536, 1792), (1792, 1920), (1920, T)]:
+            group(scopy, c0, c1)
+        group(vcopy, 0, 256)
+        group(vcopy, 256, 512)
         quantize_out(0, 256)
-        round_plane(vround, 3, 512, c0)
+        group(vcopy, 512, 768)
         quantize_out(256, 512)
         quantize_out(1024, 1280)
+        group(vcopy, 768, 1024)
         quantize_out(1280, 1536)
         nc.sync.dma_start(
             out_words.rearrange("p (side c) -> p side c", side=2)[:, :, :QUARTER],

@@ -28,8 +28,9 @@ BANK_ENTRIES = 128
 W1_VECTOR_GROUPS = 80
 
 QUARTER = T // QUADS
-MIDDLE = T // 2
+VECTOR_PLANES = (1, 2)
 LOW = 1280
+STORE_CUTS = [0, 1024, 1536, T]
 
 
 def deal_weights(copy, grouped, m0, m1, raw, raw_m0):
@@ -70,11 +71,8 @@ def tile_picked_zmae_mlprelu_po_kernel(
         word_table = keep.tile([P, T], I32, name="word_table", tag="word_table", align_bytes=ALIGN)
         nc.sync.dma_start(word_table[:], x_words[0].rearrange("p c r -> p (c r)").bitcast(I32))
 
-        w2_rows = w2.rearrange("(p j) c -> p j c", j=PACK)
-        w2_left = keep.tile([P, PACK * N // 2], F32, name="w2_left", align_bytes=ALIGN)
-        nc.sync.dma_start(w2_left[:].rearrange("p (j c) -> p j c", j=PACK), w2_rows[:, :, : N // 2])
-        w2_right = keep.tile([P, PACK * N // 2], F32, name="w2_right", align_bytes=ALIGN)
-        nc.sync.dma_start(w2_right[:].rearrange("p (j c) -> p j c", j=PACK), w2_rows[:, :, N // 2 :])
+        w2_raw = keep.tile([P, PACK * N], F32, name="w2_raw", align_bytes=ALIGN)
+        nc.sync.dma_start(w2_raw[:], w2.rearrange("(p j) c -> p (j c)", j=PACK))
 
         x_scale = keep.tile([P, S], U8, name="x_scale", align_bytes=ALIGN)
         nc.vector.tensor_copy(x_scale[:], scale_table[:].indirect(offsets[:]))
@@ -92,8 +90,7 @@ def tile_picked_zmae_mlprelu_po_kernel(
             nc.vector.tensor_copy(x_codes[:, j0 : j0 + HALF], word_table[:].bitcast(U32).indirect(entries))
 
         w2_grouped = keep.tile([P, PACK * N], BF16, name="w2_grouped", tag="word_table", align_bytes=ALIGN)
-        deal_weights(nc.vector.tensor_copy, w2_grouped, 0, P // 2, w2_left, 0)
-        deal_weights(nc.vector.tensor_copy, w2_grouped, P // 2, P, w2_right, P // 2)
+        deal_weights(nc.vector.tensor_copy, w2_grouped, 0, P, w2_raw, 0)
 
         windows = []
         for t in range(PACK):
@@ -151,10 +148,11 @@ def tile_picked_zmae_mlprelu_po_kernel(
         quantize_w2(P, 2 * P)
         quantize_w2(2 * P, N)
 
-        y_planes = []
-        for t in range(PACK):
-            y = keep.tile([P, S], F32, name=f"y{t}", tag=f"y{t}", align_bytes=ALIGN)
-            cuts = [0, HALF, last_bank, S] if t == 0 else [0, S]
+        y_planes = [keep.tile([P, S], F32, name=f"y{t}", align_bytes=ALIGN) for t in range(3)]
+        y_planes.append(y_planes[0])
+
+        def layer_two(t, cuts):
+            empty = nc.vector.tensor_copy if t in VECTOR_PLANES else nc.scalar.copy
             for j0, j1 in zip(cuts, cuts[1:]):
                 bank = psum.tile([P, j1 - j0], F32, name="bank", tag="bank")
                 nc.tensor.matmul_mx(
@@ -166,17 +164,10 @@ def tile_picked_zmae_mlprelu_po_kernel(
                     start=True,
                     stop=True,
                 )
-                nc.scalar.copy(out=y[:, j0:j1], in_=bank[:])
-            y_planes.append(y)
-
-        low = keep.tile([P, PACK * LOW], BF16, name="low", align_bytes=ALIGN)
-        out_grouped = keep.tile([P, T * PACK], BF16, name="out_grouped", align_bytes=ALIGN)
-
-        def gpsimd_copy(out, in_):
-            nc.gpsimd.tensor_scalar(out, in_, 1.0, -0.0, MULT, ADD)
+                empty(out=y_planes[t][:, j0:j1], in_=bank[:])
 
         def scatter(t):
-            if t % 2 == 0:
+            if t in VECTOR_PLANES:
                 nc.vector.tensor_copy(windows[t][:].indirect(offsets[:]), y_planes[t][:])
             else:
                 for j0 in range(0, S, HALF):
@@ -186,12 +177,30 @@ def tile_picked_zmae_mlprelu_po_kernel(
                     )
             nc.sync.dma_start(out_planes[:, t, :], windows[t][:])
 
-        for t in range(PACK):
+        layer_two(0, [0, HALF, last_bank, S])
+        layer_two(1, [0, S])
+        layer_two(2, [0, S])
+        scatter(0)
+        layer_two(3, [0, S])
+        for t in range(1, PACK):
             scatter(t)
-        high = keep.tile([P, PACK * (T - LOW)], BF16, name="high", tag="y2", align_bytes=ALIGN)
+
+        def holder(tiles, cuts, c0):
+            n = max(i for i, cut in enumerate(cuts) if cut <= c0)
+            return tiles[n], cuts[n]
+
+        rounded_cuts = [0, LOW, T]
+        rounded_tiles = [
+            keep.tile([P, PACK * (c1 - c0)], BF16, name=f"rounded{c0}", align_bytes=ALIGN)
+            for c0, c1 in zip(rounded_cuts, rounded_cuts[1:])
+        ]
+        out_grouped = keep.tile([P, T * PACK], BF16, name="out_grouped", align_bytes=ALIGN)
+
+        def gpsimd_copy(out, in_):
+            nc.gpsimd.tensor_scalar(out, in_, 1.0, -0.0, MULT, ADD)
 
         def rounded(c0, c1):
-            tile, base = (low, 0) if c0 < LOW else (high, LOW)
+            tile, base = holder(rounded_tiles, rounded_cuts, c0)
             return tile[:].rearrange("p (t c) -> p t c", t=PACK)[:, :, c0 - base : c1 - base]
 
         def round_plane(copy, t, c0, c1):
@@ -203,53 +212,55 @@ def tile_picked_zmae_mlprelu_po_kernel(
                 in_=rounded(c0, c1).rearrange("p t (c i) -> p c t i", i=PACK),
             )
 
-        for t in range(2):
-            round_plane(gpsimd_copy, t, 0, LOW)
-        round_plane(nc.vector.tensor_copy, 2, 0, LOW)
-        for t in range(3):
-            round_plane(nc.vector.tensor_copy, t, LOW, T)
-
         out_scale = keep.tile([P, QUARTER], U8, name="out_scale", align_bytes=ALIGN)
-        codes_even = keep.tile([P, 2 * QUARTER], I32, name="codes_even", align_bytes=ALIGN)
-        codes_1 = keep.tile([P, QUARTER], I32, name="codes_1", align_bytes=ALIGN)
-        codes_3 = keep.tile([P, QUARTER], I32, name="codes_3", align_bytes=ALIGN)
-        quarter_codes = [codes_even[:, :QUARTER], codes_1[:], codes_even[:, QUARTER:], codes_3[:]]
+        code_tiles = [
+            keep.tile([P, c1 - c0], I32, name=f"codes{c0}", align_bytes=ALIGN)
+            for c0, c1 in zip(STORE_CUTS, STORE_CUTS[1:])
+        ]
 
         def quantize_out(c0, c1):
             s, r = divmod(c0, QUARTER)
+            tile, base = holder(code_tiles, STORE_CUTS, c0)
             nc.vector.quantize_mx(
-                out=quarter_codes[s][:, r : r + c1 - c0].bitcast(FP8X4),
+                out=tile[:, c0 - base : c1 - base].bitcast(FP8X4),
                 scales=out_scale[4 * s :, r : r + c1 - c0],
                 in_=out_grouped[:, c0 * PACK : c1 * PACK],
             )
 
+        def store_words(c0):
+            n = STORE_CUTS.index(c0)
+            nc.sync.dma_start(out_words[:, c0 : STORE_CUTS[n + 1]], code_tiles[n][:])
+
         vcopy = nc.vector.tensor_copy
         scopy = nc.scalar.copy
-        round_plane(scopy, 3, 1024, LOW)
-        round_plane(scopy, 3, LOW, 1536)
-        round_plane(vcopy, 3, 0, 512)
-        round_plane(vcopy, 3, 512, 1024)
-        round_plane(vcopy, 3, 1536, T)
-        for c0, c1 in [(1024, 1280), (1280, 1536), (1536, 1792), (1792, 1920), (1920, T)]:
+        round_plane(gpsimd_copy, 0, 0, LOW)
+        round_plane(scopy, 0, LOW, T)
+        round_plane(gpsimd_copy, 1, 0, LOW)
+        round_plane(gpsimd_copy, 1, LOW, T)
+        round_plane(vcopy, 2, 0, LOW)
+        round_plane(vcopy, 2, LOW, T)
+
+        round_plane(scopy, 3, 0, 384)
+        round_plane(vcopy, 3, 384, LOW)
+        round_plane(vcopy, 3, LOW, T)
+        for c0, c1 in [(0, 256), (256, 512), (1536, 1792), (1792, 1920), (1920, T)]:
             group(scopy, c0, c1)
-        group(vcopy, 0, 256)
-        group(vcopy, 256, 512)
-        quantize_out(0, 256)
         group(vcopy, 512, 768)
-        quantize_out(256, 512)
-        quantize_out(1024, 1280)
         group(vcopy, 768, 1024)
+        quantize_out(0, 256)
+        quantize_out(768, 1024)
+        quantize_out(512, 768)
+        quantize_out(256, 512)
+        store_words(0)
+        group(vcopy, 1024, 1280)
+        group(vcopy, 1280, 1536)
+        quantize_out(1024, 1280)
         quantize_out(1280, 1536)
-        nc.sync.dma_start(
-            out_words.rearrange("p (side c) -> p side c", side=2)[:, :, :QUARTER],
-            codes_even[:].rearrange("p (side c) -> p side c", side=2),
-        )
-        quantize_out(512, 1024)
-        nc.sync.dma_start(out_words[:, QUARTER:MIDDLE], codes_1[:])
+        store_words(1024)
         quantize_out(1536, 1792)
         quantize_out(1792, 1920)
         quantize_out(1920, T)
-        nc.sync.dma_start(out_words[:, MIDDLE + QUARTER :], codes_3[:])
+        store_words(1536)
 
         for q in range(QUADS):
             nc.sync.dma_start(

@@ -28,9 +28,8 @@ BANK_ENTRIES = 128
 W1_VECTOR_GROUPS = 80
 
 QUARTER = T // QUADS
-VECTOR_PLANES = (1, 2)
-LOW = 1280
-STORE_CUTS = [0, 1024, 1536, T]
+VECTOR_PLANES = (1, 3)
+STORE_CUTS = [0, 1024, 1536, 1920, T]
 
 
 def deal_weights(copy, grouped, m0, m1, raw, raw_m0):
@@ -148,8 +147,10 @@ def tile_picked_zmae_mlprelu_po_kernel(
         quantize_w2(P, 2 * P)
         quantize_w2(2 * P, N)
 
-        y_planes = [keep.tile([P, S], F32, name=f"y{t}", align_bytes=ALIGN) for t in range(3)]
-        y_planes.append(y_planes[0])
+
+        rounded_tile = keep.tile([P, PACK * T], BF16, name="rounded", align_bytes=ALIGN)
+        y_planes = [keep.tile([P, S], F32, name=f"y{t}", align_bytes=ALIGN)[:] for t in (0, 2, 3)]
+        y_planes = y_planes[:1] + [rounded_tile[:, T - 2 * S : T].bitcast(F32)] + y_planes[1:]
 
         def layer_two(t, cuts):
             empty = nc.vector.tensor_copy if t in VECTOR_PLANES else nc.scalar.copy
@@ -168,7 +169,7 @@ def tile_picked_zmae_mlprelu_po_kernel(
 
         def scatter(t):
             if t in VECTOR_PLANES:
-                nc.vector.tensor_copy(windows[t][:].indirect(offsets[:]), y_planes[t][:])
+                nc.vector.tensor_copy(windows[t][:].indirect(offsets[:]), y_planes[t])
             else:
                 for j0 in range(0, S, HALF):
                     entries = offsets[:, j0 // PER_COLUMN : (j0 + HALF) // PER_COLUMN]
@@ -180,28 +181,21 @@ def tile_picked_zmae_mlprelu_po_kernel(
         layer_two(0, [0, HALF, last_bank, S])
         layer_two(1, [0, S])
         layer_two(2, [0, S])
-        scatter(0)
         layer_two(3, [0, S])
-        for t in range(1, PACK):
+        for t in range(PACK):
             scatter(t)
 
         def holder(tiles, cuts, c0):
             n = max(i for i, cut in enumerate(cuts) if cut <= c0)
             return tiles[n], cuts[n]
 
-        rounded_cuts = [0, LOW, T]
-        rounded_tiles = [
-            keep.tile([P, PACK * (c1 - c0)], BF16, name=f"rounded{c0}", align_bytes=ALIGN)
-            for c0, c1 in zip(rounded_cuts, rounded_cuts[1:])
-        ]
         out_grouped = keep.tile([P, T * PACK], BF16, name="out_grouped", align_bytes=ALIGN)
 
         def gpsimd_copy(out, in_):
             nc.gpsimd.tensor_scalar(out, in_, 1.0, -0.0, MULT, ADD)
 
         def rounded(c0, c1):
-            tile, base = holder(rounded_tiles, rounded_cuts, c0)
-            return tile[:].rearrange("p (t c) -> p t c", t=PACK)[:, :, c0 - base : c1 - base]
+            return rounded_tile[:].rearrange("p (t c) -> p t c", t=PACK)[:, :, c0:c1]
 
         def round_plane(copy, t, c0, c1):
             copy(out=rounded(c0, c1)[:, t, :], in_=windows[t][:, c0:c1])
@@ -233,16 +227,16 @@ def tile_picked_zmae_mlprelu_po_kernel(
 
         vcopy = nc.vector.tensor_copy
         scopy = nc.scalar.copy
-        round_plane(gpsimd_copy, 0, 0, LOW)
-        round_plane(scopy, 0, LOW, T)
-        round_plane(gpsimd_copy, 1, 0, LOW)
-        round_plane(gpsimd_copy, 1, LOW, T)
-        round_plane(vcopy, 2, 0, LOW)
-        round_plane(vcopy, 2, LOW, T)
+        round_plane(gpsimd_copy, 0, 0, 640)
+        round_plane(vcopy, 1, 0, 1280)
+        round_plane(gpsimd_copy, 0, 640, T)
+        round_plane(gpsimd_copy, 1, 1280, T)
+        round_plane(scopy, 2, 0, 1024)
+        round_plane(gpsimd_copy, 2, 1024, T)
 
         round_plane(scopy, 3, 0, 384)
-        round_plane(vcopy, 3, 384, LOW)
-        round_plane(vcopy, 3, LOW, T)
+        round_plane(vcopy, 3, 384, 1280)
+        round_plane(vcopy, 3, 1280, T)
         for c0, c1 in [(0, 256), (256, 512), (1536, 1792), (1792, 1920), (1920, T)]:
             group(scopy, c0, c1)
         group(vcopy, 512, 768)
@@ -259,11 +253,13 @@ def tile_picked_zmae_mlprelu_po_kernel(
         store_words(1024)
         quantize_out(1536, 1792)
         quantize_out(1792, 1920)
-        quantize_out(1920, T)
         store_words(1536)
+        quantize_out(1920, T)
+        store_words(1920)
 
         for q in range(QUADS):
-            nc.sync.dma_start(
+            queue = nc.sync if q < QUADS // 2 else nc.scalar
+            queue.dma_start(
                 out_2[0, 4 * q : 4 * q + 4, :].bitcast(I32).rearrange("r (s c) -> s r c", s=QUADS),
                 out_scale[32 * q : 32 * q + 16, :].bitcast(I32),
             )

@@ -231,8 +231,8 @@ def tile_picked_zmae_mlprelu_po_kernel(
         round_plane(vcopy, 1, 0, 1280)
         round_plane(gpsimd_copy, 0, 640, T)
         round_plane(gpsimd_copy, 1, 1280, T)
-        round_plane(scopy, 2, 0, 1024)
-        round_plane(gpsimd_copy, 2, 1024, T)
+        round_plane(scopy, 2, 0, 1152)
+        round_plane(gpsimd_copy, 2, 1152, T)
 
         round_plane(scopy, 3, 0, 384)
         round_plane(vcopy, 3, 384, 1280)

@@ -28,7 +28,7 @@ BANK_ENTRIES = 128
 W1_VECTOR_GROUPS = 80
 
 QUARTER = T // QUADS
-VECTOR_PLANES = (1, 3)
+SCALAR_SHARE_2 = 1536
 STORE_CUTS = [0, 1024, 1536, 1920, T]
 
 
@@ -147,43 +147,43 @@ def tile_picked_zmae_mlprelu_po_kernel(
         quantize_w2(P, 2 * P)
         quantize_w2(2 * P, N)
 
-
         rounded_tile = keep.tile([P, PACK * T], BF16, name="rounded", align_bytes=ALIGN)
-        y_planes = [keep.tile([P, S], F32, name=f"y{t}", align_bytes=ALIGN)[:] for t in (0, 2, 3)]
-        y_planes = y_planes[:1] + [rounded_tile[:, T - 2 * S : T].bitcast(F32)] + y_planes[1:]
+        y_planes = [keep.tile([P, S], F32, name=f"y{t}", align_bytes=ALIGN)[:] for t in range(PACK)]
 
-        def layer_two(t, cuts):
-            empty = nc.vector.tensor_copy if t in VECTOR_PLANES else nc.scalar.copy
-            for j0, j1 in zip(cuts, cuts[1:]):
-                bank = psum.tile([P, j1 - j0], F32, name="bank", tag="bank")
-                nc.tensor.matmul_mx(
-                    out=bank[:],
-                    lhsT=w2_codes[:, t * P : (t + 1) * P].bitcast(FP8X4),
-                    lhsT_scale=w2_scale[:, t * P : (t + 1) * P],
-                    rhs=h_codes[:, j0:j1].bitcast(FP8X4),
-                    rhs_scale=h_scale[:, j0:j1],
-                    start=True,
-                    stop=True,
+        def layer_two(t, j0, j1):
+            bank = psum.tile([P, j1 - j0], F32, name="bank", tag="bank")
+            nc.tensor.matmul_mx(
+                out=bank[:],
+                lhsT=w2_codes[:, t * P : (t + 1) * P].bitcast(FP8X4),
+                lhsT_scale=w2_scale[:, t * P : (t + 1) * P],
+                rhs=h_codes[:, j0:j1].bitcast(FP8X4),
+                rhs_scale=h_scale[:, j0:j1],
+                start=True,
+                stop=True,
+            )
+            return bank
+
+        def scatter_halves(t):
+            for j0 in range(0, S, HALF):
+                entries = offsets[:, j0 // PER_COLUMN : (j0 + HALF) // PER_COLUMN]
+                nc.scalar.activation(
+                    out=windows[t][:].indirect(entries), in_=y_planes[t][:, j0 : j0 + HALF], func=COPY
                 )
-                empty(out=y_planes[t][:, j0:j1], in_=bank[:])
-
-        def scatter(t):
-            if t in VECTOR_PLANES:
-                nc.vector.tensor_copy(windows[t][:].indirect(offsets[:]), y_planes[t])
-            else:
-                for j0 in range(0, S, HALF):
-                    entries = offsets[:, j0 // PER_COLUMN : (j0 + HALF) // PER_COLUMN]
-                    nc.scalar.activation(
-                        out=windows[t][:].indirect(entries), in_=y_planes[t][:, j0 : j0 + HALF], func=COPY
-                    )
             nc.sync.dma_start(out_planes[:, t, :], windows[t][:])
 
-        layer_two(0, [0, HALF, last_bank, S])
-        layer_two(1, [0, S])
-        layer_two(2, [0, S])
-        layer_two(3, [0, S])
-        for t in range(PACK):
-            scatter(t)
+        def scatter_whole(t):
+            nc.vector.tensor_copy(windows[t][:].indirect(offsets[:]), y_planes[t])
+            nc.sync.dma_start(out_planes[:, t, :], windows[t][:])
+
+        cuts = [0, HALF, last_bank, S]
+        for j0, j1 in zip(cuts, cuts[1:]):
+            nc.scalar.copy(out=y_planes[0][:, j0:j1], in_=layer_two(0, j0, j1)[:])
+        for t in range(1, PACK):
+            nc.vector.tensor_copy(out=y_planes[t], in_=layer_two(t, 0, S)[:])
+        scatter_halves(0)
+        scatter_whole(1)
+        scatter_halves(2)
+        scatter_whole(3)
 
         def holder(tiles, cuts, c0):
             n = max(i for i, cut in enumerate(cuts) if cut <= c0)
@@ -227,12 +227,10 @@ def tile_picked_zmae_mlprelu_po_kernel(
 
         vcopy = nc.vector.tensor_copy
         scopy = nc.scalar.copy
-        round_plane(gpsimd_copy, 0, 0, 640)
-        round_plane(vcopy, 1, 0, 1280)
-        round_plane(gpsimd_copy, 0, 640, T)
-        round_plane(gpsimd_copy, 1, 1280, T)
-        round_plane(scopy, 2, 0, 1152)
-        round_plane(gpsimd_copy, 2, 1152, T)
+        round_plane(gpsimd_copy, 0, 0, T)
+        round_plane(gpsimd_copy, 1, 0, T)
+        round_plane(scopy, 2, 0, SCALAR_SHARE_2)
+        round_plane(gpsimd_copy, 2, SCALAR_SHARE_2, T)
 
         round_plane(scopy, 3, 0, 384)
         round_plane(vcopy, 3, 384, 1280)

@@ -29,7 +29,7 @@ W1_VECTOR_GROUPS = 80
 
 QUARTER = T // QUADS
 SCALAR_SHARE_2 = 1536
-STORE_CUTS = [0, 1024, 1536, 1920, T]
+STORE_CUTS = [0, 1024, 1536, T]
 
 
 def deal_weights(copy, grouped, m0, m1, raw, raw_m0):
@@ -251,9 +251,8 @@ def tile_picked_zmae_mlprelu_po_kernel(
         store_words(1024)
         quantize_out(1536, 1792)
         quantize_out(1792, 1920)
-        store_words(1536)
         quantize_out(1920, T)
-        store_words(1920)
+        store_words(1536)
 
         for q in range(QUADS):
             queue = nc.sync if q < QUADS // 2 else nc.scalar

@@ -221,9 +221,9 @@ def tile_picked_zmae_mlprelu_po_kernel(
                 in_=out_grouped[:, c0 * PACK : c1 * PACK],
             )
 
-        def store_words(c0):
+        def store_words(c0, queue=nc.sync):
             n = STORE_CUTS.index(c0)
-            nc.sync.dma_start(out_words[:, c0 : STORE_CUTS[n + 1]], code_tiles[n][:])
+            queue.dma_start(out_words[:, c0 : STORE_CUTS[n + 1]], code_tiles[n][:])
 
         vcopy = nc.vector.tensor_copy
         scopy = nc.scalar.copy
@@ -252,11 +252,10 @@ def tile_picked_zmae_mlprelu_po_kernel(
         quantize_out(1536, 1792)
         quantize_out(1792, 1920)
         quantize_out(1920, T)
-        store_words(1536)
+        store_words(1536, nc.scalar)
 
         for q in range(QUADS):
-            queue = nc.sync if q < QUADS // 2 else nc.scalar
-            queue.dma_start(
+            nc.sync.dma_start(
                 out_2[0, 4 * q : 4 * q + 4, :].bitcast(I32).rearrange("r (s c) -> s r c", s=QUADS),
                 out_scale[32 * q : 32 * q + 16, :].bitcast(I32),
             )

@@ -25,6 +25,7 @@ ALIGN = 64
 PER_COLUMN = 16
 HALF = S // 2
 BANK_ENTRIES = 128
+GATHER_CUTS = [0, BANK_ENTRIES, HALF, S]
 W1_VECTOR_GROUPS = 80
 
 QUARTER = T // QUADS
@@ -84,9 +85,9 @@ def tile_picked_zmae_mlprelu_po_kernel(
         nc.vector.quantize_mx(out=w1_codes[:].bitcast(FP8X4), scales=w1_scale[:], in_=w1_grouped[:])
 
         x_codes = keep.tile([P, S], U32, name="x_codes", tag="x_codes", align_bytes=ALIGN)
-        for j0 in range(0, S, HALF):
-            entries = offsets[:, j0 // PER_COLUMN : (j0 + HALF) // PER_COLUMN]
-            nc.vector.tensor_copy(x_codes[:, j0 : j0 + HALF], word_table[:].bitcast(U32).indirect(entries))
+        for j0, j1 in zip(GATHER_CUTS, GATHER_CUTS[1:]):
+            entries = offsets[:, j0 // PER_COLUMN : j1 // PER_COLUMN]
+            nc.vector.tensor_copy(x_codes[:, j0:j1], word_table[:].bitcast(U32).indirect(entries))
 
         w2_grouped = keep.tile([P, PACK * N], BF16, name="w2_grouped", tag="word_table", align_bytes=ALIGN)
         deal_weights(nc.vector.tensor_copy, w2_grouped, 0, P, w2_raw, 0)
@@ -175,9 +176,8 @@ def tile_picked_zmae_mlprelu_po_kernel(
             nc.vector.tensor_copy(windows[t][:].indirect(offsets[:]), y_planes[t])
             nc.sync.dma_start(out_planes[:, t, :], windows[t][:])
 
-        cuts = [0, HALF, last_bank, S]
-        for j0, j1 in zip(cuts, cuts[1:]):
-            nc.scalar.copy(out=y_planes[0][:, j0:j1], in_=layer_two(0, j0, j1)[:])
+        nc.scalar.copy(out=y_planes[0][:, :HALF], in_=layer_two(0, 0, HALF)[:])
+        nc.vector.tensor_copy(out=y_planes[0][:, HALF:], in_=layer_two(0, HALF, S)[:])
         for t in range(1, PACK):
             nc.vector.tensor_copy(out=y_planes[t], in_=layer_two(t, 0, S)[:])
         scatter_halves(0)

@@ -30,7 +30,7 @@ W1_VECTOR_GROUPS = 80
 
 QUARTER = T // QUADS
 SCALAR_SHARE_2 = 1536
-STORE_CUTS = [0, 1024, 1536, T]
+STORE_CUTS = [0, 1024, 1664, T]
 
 
 def deal_weights(copy, grouped, m0, m1, raw, raw_m0):
@@ -235,7 +235,7 @@ def tile_picked_zmae_mlprelu_po_kernel(
         round_plane(scopy, 3, 0, 384)
         round_plane(vcopy, 3, 384, 1280)
         round_plane(vcopy, 3, 1280, T)
-        for c0, c1 in [(0, 256), (256, 512), (1536, 1792), (1792, 1920), (1920, T)]:
+        for c0, c1 in [(0, 256), (256, 512), (1408, 1664), (1792, 1920), (1920, T)]:
             group(scopy, c0, c1)
         group(vcopy, 512, 768)
         group(vcopy, 768, 1024)
@@ -245,14 +245,16 @@ def tile_picked_zmae_mlprelu_po_kernel(
         quantize_out(256, 512)
         store_words(0)
         group(vcopy, 1024, 1280)
-        group(vcopy, 1280, 1536)
+        group(vcopy, 1280, 1408)
         quantize_out(1024, 1280)
         quantize_out(1280, 1536)
+        quantize_out(1536, 1664)
         store_words(1024)
-        quantize_out(1536, 1792)
+        group(vcopy, 1664, 1792)
         quantize_out(1792, 1920)
+        quantize_out(1664, 1792)
         quantize_out(1920, T)
-        store_words(1536, nc.scalar)
+        store_words(1664, nc.scalar)
 
         for q in range(QUADS):
             nc.sync.dma_start(

@@ -27,6 +27,7 @@ HALF = S // 2
 BANK_ENTRIES = 128
 GATHER_CUTS = [0, BANK_ENTRIES, HALF, S]
 W1_VECTOR_GROUPS = 80
+W2_VECTOR_GROUPS = 96
 
 QUARTER = T // QUADS
 SCALAR_SHARE_2 = 1536
@@ -89,14 +90,19 @@ def tile_picked_zmae_mlprelu_po_kernel(
             entries = offsets[:, j0 // PER_COLUMN : j1 // PER_COLUMN]
             nc.vector.tensor_copy(x_codes[:, j0:j1], word_table[:].bitcast(U32).indirect(entries))
 
-        w2_grouped = keep.tile([P, PACK * N], BF16, name="w2_grouped", tag="word_table", align_bytes=ALIGN)
-        deal_weights(nc.vector.tensor_copy, w2_grouped, 0, P, w2_raw, 0)
+        w2_first = keep.tile([P, 2 * N], BF16, name="w2_first", tag="word_table", align_bytes=ALIGN)
 
-        windows = []
-        for t in range(PACK):
-            window = keep.tile([P, T], F32, name=f"window{t}", align_bytes=ALIGN)
-            nc.sync.dma_start(window[:], mask_planes[:, t, :])
-            windows.append(window)
+        def deal_pair(copy, grouped, t0, m0, m1):
+            copy(
+                out=grouped[:].rearrange("p (t m j) -> p m j t", t=2, j=PACK)[:, m0:m1],
+                in_=w2_raw[:].rearrange("p (j m t) -> p m j t", j=PACK, t=PACK)[:, m0:m1, :, t0 : t0 + 2],
+            )
+
+        deal_pair(nc.vector.tensor_copy, w2_first, 0, 0, P)
+
+        windows = [keep.tile([P, T], F32, name=f"window{t}", align_bytes=ALIGN) for t in range(PACK)]
+        for t in (0, 2, 1, 3):
+            nc.sync.dma_start(windows[t][:], mask_planes[:, t, :])
 
         h_grouped = [
             keep.tile([P, HALF * PACK], BF16, name=f"h_grouped{half}", align_bytes=ALIGN) for half in range(2)
@@ -133,28 +139,30 @@ def tile_picked_zmae_mlprelu_po_kernel(
                 in_=h_grouped[half][:, r * PACK : (r + j1 - j0) * PACK],
             )
 
-        def quantize_w2(m0, m1):
+        def quantize_w2(grouped, t0):
             nc.vector.quantize_mx(
-                out=w2_codes[:, m0:m1].bitcast(FP8X4),
-                scales=w2_scale[:, m0:m1],
-                in_=w2_grouped[:, m0 * PACK : m1 * PACK],
+                out=w2_codes[:, t0 * P : (t0 + 2) * P].bitcast(FP8X4),
+                scales=w2_scale[:, t0 * P : (t0 + 2) * P],
+                in_=grouped[:],
             )
 
         last_bank = S - BANK_ENTRIES
         quantize_h(0, HALF)
-        quantize_w2(0, P)
+        quantize_w2(w2_first, 0)
+        w2_second = keep.tile([P, 2 * N], BF16, name="w2_second", tag="x_codes", align_bytes=ALIGN)
+        deal_pair(nc.vector.tensor_copy, w2_second, 2, 0, W2_VECTOR_GROUPS)
+        deal_pair(nc.scalar.copy, w2_second, 2, W2_VECTOR_GROUPS, P)
         quantize_h(HALF, last_bank)
         quantize_h(last_bank, S)
-        quantize_w2(P, 2 * P)
-        quantize_w2(2 * P, N)
+        quantize_w2(w2_second, 2)
 
         rounded_tile = keep.tile([P, PACK * T], BF16, name="rounded", align_bytes=ALIGN)
-        y_planes = [keep.tile([P, S], F32, name=f"y{t}", align_bytes=ALIGN)[:] for t in range(PACK)]
+        y_halves = [keep.tile([P, 2, HALF], F32, name=f"y_half{half}", align_bytes=ALIGN) for half in range(2)]
+        y_planes = {t: keep.tile([P, S], F32, name=f"y{t}", align_bytes=ALIGN) for t in (2, 3)}
 
-        def layer_two(t, j0, j1):
-            bank = psum.tile([P, j1 - j0], F32, name="bank", tag="bank")
+        def layer_two(out, t, j0, j1):
             nc.tensor.matmul_mx(
-                out=bank[:],
+                out=out,
                 lhsT=w2_codes[:, t * P : (t + 1) * P].bitcast(FP8X4),
                 lhsT_scale=w2_scale[:, t * P : (t + 1) * P],
                 rhs=h_codes[:, j0:j1].bitcast(FP8X4),
@@ -162,27 +170,32 @@ def tile_picked_zmae_mlprelu_po_kernel(
                 start=True,
                 stop=True,
             )
-            return bank
 
         def scatter_halves(t):
-            for j0 in range(0, S, HALF):
-                entries = offsets[:, j0 // PER_COLUMN : (j0 + HALF) // PER_COLUMN]
-                nc.scalar.activation(
-                    out=windows[t][:].indirect(entries), in_=y_planes[t][:, j0 : j0 + HALF], func=COPY
-                )
+            for half in range(2):
+                entries = offsets[:, half * HALF // PER_COLUMN : (half + 1) * HALF // PER_COLUMN]
+                nc.scalar.activation(out=windows[t][:].indirect(entries), in_=y_halves[half][:, t, :], func=COPY)
             nc.sync.dma_start(out_planes[:, t, :], windows[t][:])
 
         def scatter_whole(t):
-            nc.vector.tensor_copy(windows[t][:].indirect(offsets[:]), y_planes[t])
+            nc.vector.tensor_copy(windows[t][:].indirect(offsets[:]), y_planes[t][:])
             nc.sync.dma_start(out_planes[:, t, :], windows[t][:])
 
-        nc.scalar.copy(out=y_planes[0][:, :HALF], in_=layer_two(0, 0, HALF)[:])
-        nc.vector.tensor_copy(out=y_planes[0][:, HALF:], in_=layer_two(0, HALF, S)[:])
-        for t in range(1, PACK):
-            nc.vector.tensor_copy(out=y_planes[t], in_=layer_two(t, 0, S)[:])
+        for t in range(2):
+            bank = psum.tile([P, HALF], F32, name="bank", tag="bank")
+            layer_two(bank[:], t, 0, HALF)
+            nc.scalar.copy(out=y_halves[0][:, t, :], in_=bank[:])
+        bank = psum.tile([P, 2, HALF], F32, name="bank", tag="bank")
+        for t in range(2):
+            layer_two(bank[:, t, :], t, HALF, S)
+        nc.vector.tensor_copy(out=y_halves[1][:], in_=bank[:])
+        for t in (2, 3):
+            bank = psum.tile([P, S], F32, name="bank", tag="bank")
+            layer_two(bank[:], t, 0, S)
+            nc.vector.tensor_copy(out=y_planes[t][:], in_=bank[:])
         scatter_halves(0)
-        scatter_whole(1)
-        scatter_halves(2)
+        scatter_whole(2)
+        scatter_halves(1)
         scatter_whole(3)
 
         def holder(tiles, cuts, c0):
@@ -228,9 +241,9 @@ def tile_picked_zmae_mlprelu_po_kernel(
         vcopy = nc.vector.tensor_copy
         scopy = nc.scalar.copy
         round_plane(gpsimd_copy, 0, 0, T)
-        round_plane(gpsimd_copy, 1, 0, T)
-        round_plane(scopy, 2, 0, SCALAR_SHARE_2)
-        round_plane(gpsimd_copy, 2, SCALAR_SHARE_2, T)
+        round_plane(gpsimd_copy, 2, 0, T)
+        round_plane(scopy, 1, 0, SCALAR_SHARE_2)
+        round_plane(gpsimd_copy, 1, SCALAR_SHARE_2, T)
 
         round_plane(scopy, 3, 0, 384)
         round_plane(vcopy, 3, 384, 1280)

@@ -27,6 +27,7 @@ HALF = S // 2
 BANK_ENTRIES = 128
 GATHER_CUTS = [0, BANK_ENTRIES, HALF, S]
 W1_VECTOR_GROUPS = 80
+W2_FILL_GROUPS = 40
 W2_VECTOR_GROUPS = 96
 
 QUARTER = T // QUADS
@@ -58,10 +59,10 @@ def tile_picked_zmae_mlprelu_po_kernel(
         scale_rows = keep.tile([P, T], U8, name="scale_rows", align_bytes=ALIGN)
         scale_table = keep.tile([P, T], U8, name="scale_table", align_bytes=ALIGN)
         nc.vector.memset(scale_table[:].bitcast(I32), 0)
-        for q in range(QUADS):
-            rows = slice(32 * q, 32 * q + 4)
-            queue = nc.sync if q < QUADS // 2 else nc.scalar
-            queue.dma_start(scale_rows[rows, :].bitcast(I32), x_scales[0, 4 * q : 4 * q + 4, :].bitcast(I32))
+        for half in range(2):
+            rows = slice(64 * half, 64 * half + 8)
+            queue = nc.sync if half == 0 else nc.scalar
+            queue.dma_start(scale_rows[rows, :].bitcast(I32), x_scales[0, 8 * half : 8 * half + 8, :].bitcast(I32))
             nc.vector.tensor_copy(scale_table[rows, :].bitcast(I32), scale_rows[rows, :].bitcast(I32))
 
         nc.sync.dma_start(offsets[:], offs)
@@ -72,11 +73,20 @@ def tile_picked_zmae_mlprelu_po_kernel(
         word_table = keep.tile([P, T], I32, name="word_table", tag="word_table", align_bytes=ALIGN)
         nc.sync.dma_start(word_table[:], x_words[0].rearrange("p c r -> p (c r)").bitcast(I32))
 
+        picked_scale = keep.tile([P, S], U8, name="picked_scale", align_bytes=ALIGN)
+        nc.vector.tensor_copy(picked_scale[:], scale_table[:].indirect(offsets[:]))
+        x_scale = keep.tile([P, S], U8, name="x_scale", align_bytes=ALIGN)
+        for first in (0, 64):
+            nc.vector.tensor_copy(
+                x_scale[first : first + 4, :].bitcast(I32), picked_scale[first : first + 4, :].bitcast(I32)
+            )
+        for first in (0, 64):
+            nc.sync.dma_start(
+                x_scale[first + 32 : first + 36, :].bitcast(I32), picked_scale[first + 4 : first + 8, :].bitcast(I32)
+            )
+
         w2_raw = keep.tile([P, PACK * N], F32, name="w2_raw", align_bytes=ALIGN)
         nc.sync.dma_start(w2_raw[:], w2.rearrange("(p j) c -> p (j c)", j=PACK))
-
-        x_scale = keep.tile([P, S], U8, name="x_scale", align_bytes=ALIGN)
-        nc.vector.tensor_copy(x_scale[:], scale_table[:].indirect(offsets[:]))
 
         w1_grouped = keep.tile([P, PACK * H], BF16, name="w1_grouped", tag="x_codes", align_bytes=ALIGN)
         deal_weights(nc.vector.tensor_copy, w1_grouped, 0, W1_VECTOR_GROUPS, w1_raw, 0)
@@ -90,25 +100,29 @@ def tile_picked_zmae_mlprelu_po_kernel(
             entries = offsets[:, j0 // PER_COLUMN : j1 // PER_COLUMN]
             nc.vector.tensor_copy(x_codes[:, j0:j1], word_table[:].bitcast(U32).indirect(entries))
 
-        w2_first = keep.tile([P, 2 * N], BF16, name="w2_first", tag="word_table", align_bytes=ALIGN)
+        grouped = keep.tile([P, (N + S) * PACK], BF16, name="grouped", align_bytes=ALIGN)
+        codes = keep.tile([P, N + S], U32, name="codes", align_bytes=ALIGN)
+        scale = keep.tile([P, N + S], U8, name="scale", align_bytes=ALIGN)
+        h_first = [HALF + 2 * P, 0]
 
-        def deal_pair(copy, grouped, t0, m0, m1):
+        def plane_first(t):
+            return t * P + HALF if t < 2 else t * P + S
+
+        def deal_pair(copy, t0, m0, m1):
+            first = plane_first(t0) * PACK
             copy(
-                out=grouped[:].rearrange("p (t m j) -> p m j t", t=2, j=PACK)[:, m0:m1],
+                out=grouped[:, first : first + 2 * N].rearrange("p (t m j) -> p m j t", t=2, j=PACK)[:, m0:m1],
                 in_=w2_raw[:].rearrange("p (j m t) -> p m j t", j=PACK, t=PACK)[:, m0:m1, :, t0 : t0 + 2],
             )
 
-        deal_pair(nc.vector.tensor_copy, w2_first, 0, 0, P)
+        deal_pair(nc.vector.tensor_copy, 0, 0, P)
 
         windows = [keep.tile([P, T], F32, name=f"window{t}", align_bytes=ALIGN) for t in range(PACK)]
-        for t in (0, 2, 1, 3):
+        for t in (1, 2, 0, 3):
             nc.sync.dma_start(windows[t][:], mask_planes[:, t, :])
 
-        h_grouped = [
-            keep.tile([P, HALF * PACK], BF16, name=f"h_grouped{half}", align_bytes=ALIGN) for half in range(2)
-        ]
         for j0 in range(0, S, BANK_ENTRIES):
-            half, r = divmod(j0, HALF)
+            r = h_first[j0 // HALF] + j0 % HALF
             bank = psum.tile([P, PACK, BANK_ENTRIES], F32, name="bank", tag="bank")
             for t in range(PACK):
                 nc.tensor.matmul_mx(
@@ -121,52 +135,33 @@ def tile_picked_zmae_mlprelu_po_kernel(
                     stop=True,
                 )
             nc.scalar.activation(
-                out=h_grouped[half][:, r * PACK : (r + BANK_ENTRIES) * PACK].rearrange("p (n t) -> p n t", t=PACK),
+                out=grouped[:, r * PACK : (r + BANK_ENTRIES) * PACK].rearrange("p (n t) -> p n t", t=PACK),
                 in_=bank[:].rearrange("p t n -> p n t"),
                 func=RELU,
             )
 
-        h_codes = keep.tile([P, S], U32, name="h_codes", align_bytes=ALIGN)
-        h_scale = keep.tile([P, S], U8, name="h_scale", align_bytes=ALIGN)
-        w2_codes = keep.tile([P, N], U32, name="w2_codes", align_bytes=ALIGN)
-        w2_scale = keep.tile([P, N], U8, name="w2_scale", align_bytes=ALIGN)
-
-        def quantize_h(j0, j1):
-            half, r = divmod(j0, HALF)
+        def quantize(c0, c1):
             nc.vector.quantize_mx(
-                out=h_codes[:, j0:j1].bitcast(FP8X4),
-                scales=h_scale[:, j0:j1],
-                in_=h_grouped[half][:, r * PACK : (r + j1 - j0) * PACK],
+                out=codes[:, c0:c1].bitcast(FP8X4), scales=scale[:, c0:c1], in_=grouped[:, c0 * PACK : c1 * PACK]
             )
 
-        def quantize_w2(grouped, t0):
-            nc.vector.quantize_mx(
-                out=w2_codes[:, t0 * P : (t0 + 2) * P].bitcast(FP8X4),
-                scales=w2_scale[:, t0 * P : (t0 + 2) * P],
-                in_=grouped[:],
-            )
-
-        last_bank = S - BANK_ENTRIES
-        quantize_h(0, HALF)
-        quantize_w2(w2_first, 0)
-        w2_second = keep.tile([P, 2 * N], BF16, name="w2_second", tag="x_codes", align_bytes=ALIGN)
-        deal_pair(nc.vector.tensor_copy, w2_second, 2, 0, W2_VECTOR_GROUPS)
-        deal_pair(nc.scalar.copy, w2_second, 2, W2_VECTOR_GROUPS, P)
-        quantize_h(HALF, last_bank)
-        quantize_h(last_bank, S)
-        quantize_w2(w2_second, 2)
+        quantize(plane_first(1), plane_first(2))
+        quantize(0, plane_first(1))
+        deal_pair(nc.vector.tensor_copy, 2, 0, W2_FILL_GROUPS)
+        deal_pair(nc.vector.tensor_copy, 2, W2_FILL_GROUPS, W2_VECTOR_GROUPS)
+        deal_pair(nc.scalar.copy, 2, W2_VECTOR_GROUPS, P)
+        quantize(plane_first(2), N + S)
 
         rounded_tile = keep.tile([P, PACK * T], BF16, name="rounded", align_bytes=ALIGN)
-        y_halves = [keep.tile([P, 2, HALF], F32, name=f"y_half{half}", align_bytes=ALIGN) for half in range(2)]
-        y_planes = {t: keep.tile([P, S], F32, name=f"y{t}", align_bytes=ALIGN) for t in (2, 3)}
+        y_planes = [keep.tile([P, S], F32, name=f"y{t}", align_bytes=ALIGN) for t in range(PACK)]
 
-        def layer_two(out, t, j0, j1):
+        def layer_two(out, t, half):
             nc.tensor.matmul_mx(
                 out=out,
-                lhsT=w2_codes[:, t * P : (t + 1) * P].bitcast(FP8X4),
-                lhsT_scale=w2_scale[:, t * P : (t + 1) * P],
-                rhs=h_codes[:, j0:j1].bitcast(FP8X4),
-                rhs_scale=h_scale[:, j0:j1],
+                lhsT=codes[:, plane_first(t) : plane_first(t) + P].bitcast(FP8X4),
+                lhsT_scale=scale[:, plane_first(t) : plane_first(t) + P],
+                rhs=codes[:, h_first[half] : h_first[half] + HALF].bitcast(FP8X4),
+                rhs_scale=scale[:, h_first[half] : h_first[half] + HALF],
                 start=True,
                 stop=True,
             )
@@ -174,28 +169,25 @@ def tile_picked_zmae_mlprelu_po_kernel(
         def scatter_halves(t):
             for half in range(2):
                 entries = offsets[:, half * HALF // PER_COLUMN : (half + 1) * HALF // PER_COLUMN]
-                nc.scalar.activation(out=windows[t][:].indirect(entries), in_=y_halves[half][:, t, :], func=COPY)
+                nc.scalar.activation(out=windows[t][:].indirect(entries), in_=y_planes[t][:, half * HALF : (half + 1) * HALF], func=COPY)
             nc.sync.dma_start(out_planes[:, t, :], windows[t][:])
 
         def scatter_whole(t):
             nc.vector.tensor_copy(windows[t][:].indirect(offsets[:]), y_planes[t][:])
             nc.sync.dma_start(out_planes[:, t, :], windows[t][:])
 
-        for t in range(2):
+        for half, copy in enumerate([nc.scalar.copy, nc.vector.tensor_copy]):
             bank = psum.tile([P, HALF], F32, name="bank", tag="bank")
-            layer_two(bank[:], t, 0, HALF)
-            nc.scalar.copy(out=y_halves[0][:, t, :], in_=bank[:])
-        bank = psum.tile([P, 2, HALF], F32, name="bank", tag="bank")
-        for t in range(2):
-            layer_two(bank[:, t, :], t, HALF, S)
-        nc.vector.tensor_copy(out=y_halves[1][:], in_=bank[:])
-        for t in (2, 3):
+            layer_two(bank[:], 1, half)
+            copy(out=y_planes[1][:, half * HALF : (half + 1) * HALF], in_=bank[:])
+        for t in (0, 2, 3):
             bank = psum.tile([P, S], F32, name="bank", tag="bank")
-            layer_two(bank[:], t, 0, S)
+            for half in range(2):
+                layer_two(bank[:, half * HALF : (half + 1) * HALF], t, half)
             nc.vector.tensor_copy(out=y_planes[t][:], in_=bank[:])
-        scatter_halves(0)
-        scatter_whole(2)
         scatter_halves(1)
+        scatter_whole(2)
+        scatter_halves(0)
         scatter_whole(3)
 
         def holder(tiles, cuts, c0):
@@ -240,10 +232,10 @@ def tile_picked_zmae_mlprelu_po_kernel(
 
         vcopy = nc.vector.tensor_copy
         scopy = nc.scalar.copy
-        round_plane(gpsimd_copy, 0, 0, T)
+        round_plane(gpsimd_copy, 1, 0, T)
         round_plane(gpsimd_copy, 2, 0, T)
-        round_plane(scopy, 1, 0, SCALAR_SHARE_2)
-        round_plane(gpsimd_copy, 1, SCALAR_SHARE_2, T)
+        round_plane(scopy, 0, 0, SCALAR_SHARE_2)
+        round_plane(gpsimd_copy, 0, SCALAR_SHARE_2, T)
 
         round_plane(scopy, 3, 0, 384)
         round_plane(vcopy, 3, 384, 1280)

@@ -30,6 +30,7 @@ W1_VECTOR_GROUPS = 80
 W2_FILL_GROUPS = 40
 W2_VECTOR_GROUPS = 96
 
+BLOCK = 64
 QUARTER = T // QUADS
 SCALAR_SHARE_2 = 1536
 STORE_CUTS = [0, 1024, 1664, T]
@@ -117,8 +118,9 @@ def tile_picked_zmae_mlprelu_po_kernel(
 
         deal_pair(nc.vector.tensor_copy, 0, 0, P)
 
-        windows = [keep.tile([P, T], F32, name=f"window{t}", align_bytes=ALIGN) for t in range(PACK)]
+        windows = {}
         for t in (1, 2, 0, 3):
+            windows[t] = keep.tile([P, T], F32, name=f"window{t}", align_bytes=ALIGN)
             nc.sync.dma_start(windows[t][:], mask_planes[:, t, :])
 
         for j0 in range(0, S, BANK_ENTRIES):
@@ -176,16 +178,24 @@ def tile_picked_zmae_mlprelu_po_kernel(
             nc.vector.tensor_copy(windows[t][:].indirect(offsets[:]), y_planes[t][:])
             nc.sync.dma_start(out_planes[:, t, :], windows[t][:])
 
-        for half, copy in enumerate([nc.scalar.copy, nc.vector.tensor_copy]):
+        def half_plane(copy, t, half):
             bank = psum.tile([P, HALF], F32, name="bank", tag="bank")
-            layer_two(bank[:], 1, half)
-            copy(out=y_planes[1][:, half * HALF : (half + 1) * HALF], in_=bank[:])
-        for t in (0, 2, 3):
+            layer_two(bank[:], t, half)
+            copy(out=y_planes[t][:, half * HALF : (half + 1) * HALF], in_=bank[:])
+
+        def whole_plane(copy, t):
             bank = psum.tile([P, S], F32, name="bank", tag="bank")
             for half in range(2):
                 layer_two(bank[:, half * HALF : (half + 1) * HALF], t, half)
-            nc.vector.tensor_copy(out=y_planes[t][:], in_=bank[:])
+            copy(out=y_planes[t][:], in_=bank[:])
+
+        half_plane(nc.scalar.copy, 1, 0)
+        half_plane(nc.vector.tensor_copy, 1, 1)
+        half_plane(nc.vector.tensor_copy, 0, 1)
+        whole_plane(nc.vector.tensor_copy, 2)
         scatter_halves(1)
+        whole_plane(nc.scalar.copy, 3)
+        half_plane(nc.vector.tensor_copy, 0, 0)
         scatter_whole(2)
         scatter_halves(0)
         scatter_whole(3)
@@ -200,15 +210,23 @@ def tile_picked_zmae_mlprelu_po_kernel(
             nc.gpsimd.tensor_scalar(out, in_, 1.0, -0.0, MULT, ADD)
 
         def rounded(c0, c1):
-            return rounded_tile[:].rearrange("p (t c) -> p t c", t=PACK)[:, :, c0:c1]
+            blocks = rounded_tile[:].rearrange("p (b t c) -> p b t c", t=PACK, c=BLOCK)
+            return blocks[:, c0 // BLOCK : c1 // BLOCK]
 
         def round_plane(copy, t, c0, c1):
-            copy(out=rounded(c0, c1)[:, t, :], in_=windows[t][:, c0:c1])
+            copy(out=rounded(c0, c1)[:, :, t, :], in_=windows[t][:, c0:c1].rearrange("p (b c) -> p b c", c=BLOCK))
 
-        def group(copy, c0, c1):
+        def group(copy, c0, c1, planes=PACK):
+            out = out_grouped[:, c0 * PACK : c1 * PACK].rearrange(
+                "p (b c i t) -> p b c t i", c=BLOCK // PACK, i=PACK, t=PACK
+            )
+            in_ = rounded(c0, c1).rearrange("p b t (c i) -> p b c t i", i=PACK)
+            copy(out=out[:, :, :, :planes], in_=in_[:, :, :, :planes])
+
+        def place_last(copy, c0, c1):
             copy(
-                out=out_grouped[:, c0 * PACK : c1 * PACK].rearrange("p (c i t) -> p c t i", i=PACK, t=PACK),
-                in_=rounded(c0, c1).rearrange("p t (c i) -> p c t i", i=PACK),
+                out=out_grouped[:, c0 * PACK : c1 * PACK].rearrange("p (c t) -> p c t", t=PACK)[:, :, 3],
+                in_=windows[3][:, c0:c1],
             )
 
         out_scale = keep.tile([P, QUARTER], U8, name="out_scale", align_bytes=ALIGN)
@@ -233,14 +251,18 @@ def tile_picked_zmae_mlprelu_po_kernel(
         vcopy = nc.vector.tensor_copy
         scopy = nc.scalar.copy
         round_plane(gpsimd_copy, 1, 0, T)
-        round_plane(gpsimd_copy, 2, 0, T)
-        round_plane(scopy, 0, 0, SCALAR_SHARE_2)
-        round_plane(gpsimd_copy, 0, SCALAR_SHARE_2, T)
+        round_plane(vcopy, 2, 0, 448)
+        round_plane(gpsimd_copy, 2, 448, T)
+        round_plane(scopy, 0, 0, 128)
+        round_plane(scopy, 0, 128, 1280)
+        round_plane(gpsimd_copy, 0, 1280, T)
+        group(scopy, 0, 128, 3)
 
-        round_plane(scopy, 3, 0, 384)
-        round_plane(vcopy, 3, 384, 1280)
+        place_last(scopy, 0, 128)
+        round_plane(vcopy, 3, 128, 512)
+        round_plane(vcopy, 3, 512, 1280)
         round_plane(vcopy, 3, 1280, T)
-        for c0, c1 in [(0, 256), (256, 512), (1408, 1664), (1792, 1920), (1920, T)]:
+        for c0, c1 in [(128, 256), (256, 512), (1280, 1664), (1792, 1920), (1920, T)]:
             group(scopy, c0, c1)
         group(vcopy, 512, 768)
         group(vcopy, 768, 1024)
@@ -250,14 +272,13 @@ def tile_picked_zmae_mlprelu_po_kernel(
         quantize_out(256, 512)
         store_words(0)
         group(vcopy, 1024, 1280)
-        group(vcopy, 1280, 1408)
+        group(vcopy, 1664, 1792)
         quantize_out(1024, 1280)
         quantize_out(1280, 1536)
         quantize_out(1536, 1664)
         store_words(1024)
-        group(vcopy, 1664, 1792)
-        quantize_out(1792, 1920)
         quantize_out(1664, 1792)
+        quantize_out(1792, 1920)
         quantize_out(1920, T)
         store_words(1664, nc.scalar)
 

from contextlib import ExitStack

import concourse.mybir as mybir

K, T, S, H, N = 512, 2048, 512, 512, 512
FLOPS = 2 * K * H * S + 2 * H * N * S

F32 = mybir.dt.float32
BF16 = mybir.dt.bfloat16
I32 = mybir.dt.int32
U32 = mybir.dt.uint32
U16 = mybir.dt.uint16
U8 = mybir.dt.uint8
FP8X4 = mybir.dt.float8_e4m3fn_x4
RELU = mybir.ActivationFunctionType.Relu
COPY = mybir.ActivationFunctionType.Copy
MULT = mybir.AluOpType.mult
ADD = mybir.AluOpType.add

P = 128
PACK = 4
QUADS = 4
PSUM_BANKS = 8
ALIGN = 64
PER_COLUMN = 16
HALF = S // 2
BANK_ENTRIES = 128
GATHER_CUTS = [0, BANK_ENTRIES, HALF, S]
W1_VECTOR_GROUPS = 80
W2_FILL_GROUPS = 40
W2_VECTOR_GROUPS = 96

BLOCK = 64
QUARTER = T // QUADS
SCALAR_SHARE_2 = 1536
STORE_CUTS = [0, 1024, 1664, T]


def deal_weights(copy, grouped, m0, m1, raw, raw_m0):
    copy(
        out=grouped[:].rearrange("p (t m j) -> p m j t", t=PACK, j=PACK)[:, m0:m1],
        in_=raw[:].rearrange("p (j m t) -> p m j t", j=PACK, t=PACK)[:, m0 - raw_m0 : m1 - raw_m0],
    )


def tile_picked_zmae_mlprelu_po_kernel(
    tc, x_words, x_scales, mask, w1, w2, offs, out_0, out_1, out_2
):
    nc = tc.nc
    mask_planes = mask.rearrange("(p t) c -> p t c", t=PACK)
    out_planes = out_0.rearrange("(p t) c -> p t c", t=PACK)
    out_words = out_1[0].rearrange("p c r -> p (c r)").bitcast(I32)

    with ExitStack() as ctx:
        keep = ctx.enter_context(tc.tile_pool(name="keep", bufs=1))
        psum = ctx.enter_context(tc.psum_pool(name="psum", bufs=PSUM_BANKS))

        offsets = keep.tile([P, S // PER_COLUMN], U16, name="offsets")

        scale_rows = keep.tile([P, T], U8, name="scale_rows", align_bytes=ALIGN)
        scale_table = keep.tile([P, T], U8, name="scale_table", align_bytes=ALIGN)
        nc.vector.memset(scale_table[:].bitcast(I32), 0)
        for half in range(2):
            rows = slice(64 * half, 64 * half + 8)
            queue = nc.sync if half == 0 else nc.scalar
            queue.dma_start(scale_rows[rows, :].bitcast(I32), x_scales[0, 8 * half : 8 * half + 8, :].bitcast(I32))
            nc.vector.tensor_copy(scale_table[rows, :].bitcast(I32), scale_rows[rows, :].bitcast(I32))

        nc.sync.dma_start(offsets[:], offs)

        w1_raw = keep.tile([P, PACK * H], F32, name="w1_raw", align_bytes=ALIGN)
        nc.sync.dma_start(w1_raw[:], w1.rearrange("(p j) c -> p (j c)", j=PACK))

        word_table = keep.tile([P, T], I32, name="word_table", tag="word_table", align_bytes=ALIGN)
        nc.sync.dma_start(word_table[:], x_words[0].rearrange("p c r -> p (c r)").bitcast(I32))

        picked_scale = keep.tile([P, S], U8, name="picked_scale", align_bytes=ALIGN)
        nc.vector.tensor_copy(picked_scale[:], scale_table[:].indirect(offsets[:]))
        x_scale = keep.tile([P, S], U8, name="x_scale", align_bytes=ALIGN)
        for first in (0, 64):
            nc.vector.tensor_copy(
                x_scale[first : first + 4, :].bitcast(I32), picked_scale[first : first + 4, :].bitcast(I32)
            )
        for first in (0, 64):
            nc.sync.dma_start(
                x_scale[first + 32 : first + 36, :].bitcast(I32), picked_scale[first + 4 : first + 8, :].bitcast(I32)
            )

        w2_raw = keep.tile([P, PACK * N], F32, name="w2_raw", align_bytes=ALIGN)
        nc.sync.dma_start(w2_raw[:], w2.rearrange("(p j) c -> p (j c)", j=PACK))

        w1_grouped = keep.tile([P, PACK * H], BF16, name="w1_grouped", tag="x_codes", align_bytes=ALIGN)
        deal_weights(nc.vector.tensor_copy, w1_grouped, 0, W1_VECTOR_GROUPS, w1_raw, 0)
        deal_weights(nc.scalar.copy, w1_grouped, W1_VECTOR_GROUPS, P, w1_raw, 0)
        w1_codes = keep.tile([P, H], U32, name="w1_codes", align_bytes=ALIGN)
        w1_scale = keep.tile([P, H], U8, name="w1_scale", align_bytes=ALIGN)
        nc.vector.quantize_mx(out=w1_codes[:].bitcast(FP8X4), scales=w1_scale[:], in_=w1_grouped[:])

        x_codes = keep.tile([P, S], U32, name="x_codes", tag="x_codes", align_bytes=ALIGN)
        for j0, j1 in zip(GATHER_CUTS, GATHER_CUTS[1:]):
            entries = offsets[:, j0 // PER_COLUMN : j1 // PER_COLUMN]
            nc.vector.tensor_copy(x_codes[:, j0:j1], word_table[:].bitcast(U32).indirect(entries))

        grouped = keep.tile([P, (N + S) * PACK], BF16, name="grouped", align_bytes=ALIGN)
        codes = keep.tile([P, N + S], U32, name="codes", align_bytes=ALIGN)
        scale = keep.tile([P, N + S], U8, name="scale", align_bytes=ALIGN)
        h_first = [HALF + 2 * P, 0]

        def plane_first(t):
            return t * P + HALF if t < 2 else t * P + S

        def deal_pair(copy, t0, m0, m1):
            first = plane_first(t0) * PACK
            copy(
                out=grouped[:, first : first + 2 * N].rearrange("p (t m j) -> p m j t", t=2, j=PACK)[:, m0:m1],
                in_=w2_raw[:].rearrange("p (j m t) -> p m j t", j=PACK, t=PACK)[:, m0:m1, :, t0 : t0 + 2],
            )

        deal_pair(nc.vector.tensor_copy, 0, 0, P)

        windows = {}
        for t in (1, 2, 0, 3):
            windows[t] = keep.tile([P, T], F32, name=f"window{t}", align_bytes=ALIGN)
            nc.sync.dma_start(windows[t][:], mask_planes[:, t, :])

        for j0 in range(0, S, BANK_ENTRIES):
            r = h_first[j0 // HALF] + j0 % HALF
            bank = psum.tile([P, PACK, BANK_ENTRIES], F32, name="bank", tag="bank")
            for t in range(PACK):
                nc.tensor.matmul_mx(
                    out=bank[:, t, :],
                    lhsT=w1_codes[:, t * P : (t + 1) * P].bitcast(FP8X4),
                    lhsT_scale=w1_scale[:, t * P : (t + 1) * P],
                    rhs=x_codes[:, j0 : j0 + BANK_ENTRIES].bitcast(FP8X4),
                    rhs_scale=x_scale[:, j0 : j0 + BANK_ENTRIES],
                    start=True,
                    stop=True,
                )
            nc.scalar.activation(
                out=grouped[:, r * PACK : (r + BANK_ENTRIES) * PACK].rearrange("p (n t) -> p n t", t=PACK),
                in_=bank[:].rearrange("p t n -> p n t"),
                func=RELU,
            )

        def quantize(c0, c1):
            nc.vector.quantize_mx(
                out=codes[:, c0:c1].bitcast(FP8X4), scales=scale[:, c0:c1], in_=grouped[:, c0 * PACK : c1 * PACK]
            )

        quantize(plane_first(1), plane_first(2))
        quantize(0, plane_first(1))
        deal_pair(nc.vector.tensor_copy, 2, 0, W2_FILL_GROUPS)
        deal_pair(nc.vector.tensor_copy, 2, W2_FILL_GROUPS, W2_VECTOR_GROUPS)
        deal_pair(nc.scalar.copy, 2, W2_VECTOR_GROUPS, P)
        quantize(plane_first(2), N + S)

        rounded_tile = keep.tile([P, PACK * T], BF16, name="rounded", align_bytes=ALIGN)
        y_planes = [keep.tile([P, S], F32, name=f"y{t}", align_bytes=ALIGN) for t in range(PACK)]

        def layer_two(out, t, half):
            nc.tensor.matmul_mx(
                out=out,
                lhsT=codes[:, plane_first(t) : plane_first(t) + P].bitcast(FP8X4),
                lhsT_scale=scale[:, plane_first(t) : plane_first(t) + P],
                rhs=codes[:, h_first[half] : h_first[half] + HALF].bitcast(FP8X4),
                rhs_scale=scale[:, h_first[half] : h_first[half] + HALF],
                start=True,
                stop=True,
            )

        def scatter_halves(t):
            for half in range(2):
                entries = offsets[:, half * HALF // PER_COLUMN : (half + 1) * HALF // PER_COLUMN]
                nc.scalar.activation(out=windows[t][:].indirect(entries), in_=y_planes[t][:, half * HALF : (half + 1) * HALF], func=COPY)
            nc.sync.dma_start(out_planes[:, t, :], windows[t][:])

        def scatter_whole(t):
            nc.vector.tensor_copy(windows[t][:].indirect(offsets[:]), y_planes[t][:])
            nc.sync.dma_start(out_planes[:, t, :], windows[t][:])

        def half_plane(copy, t, half):
            bank = psum.tile([P, HALF], F32, name="bank", tag="bank")
            layer_two(bank[:], t, half)
            copy(out=y_planes[t][:, half * HALF : (half + 1) * HALF], in_=bank[:])

        def whole_plane(copy, t):
            bank = psum.tile([P, S], F32, name="bank", tag="bank")
            for half in range(2):
                layer_two(bank[:, half * HALF : (half + 1) * HALF], t, half)
            copy(out=y_planes[t][:], in_=bank[:])

        half_plane(nc.scalar.copy, 1, 0)
        half_plane(nc.vector.tensor_copy, 1, 1)
        half_plane(nc.vector.tensor_copy, 0, 1)
        whole_plane(nc.vector.tensor_copy, 2)
        scatter_halves(1)
        whole_plane(nc.scalar.copy, 3)
        half_plane(nc.vector.tensor_copy, 0, 0)
        scatter_whole(2)
        scatter_halves(0)
        scatter_whole(3)

        def holder(tiles, cuts, c0):
            n = max(i for i, cut in enumerate(cuts) if cut <= c0)
            return tiles[n], cuts[n]

        out_grouped = keep.tile([P, T * PACK], BF16, name="out_grouped", align_bytes=ALIGN)

        def gpsimd_copy(out, in_):
            nc.gpsimd.tensor_scalar(out, in_, 1.0, -0.0, MULT, ADD)

        def rounded(c0, c1):
            blocks = rounded_tile[:].rearrange("p (b t c) -> p b t c", t=PACK, c=BLOCK)
            return blocks[:, c0 // BLOCK : c1 // BLOCK]

        def round_plane(copy, t, c0, c1):
            copy(out=rounded(c0, c1)[:, :, t, :], in_=windows[t][:, c0:c1].rearrange("p (b c) -> p b c", c=BLOCK))

        def group(copy, c0, c1, planes=PACK):
            out = out_grouped[:, c0 * PACK : c1 * PACK].rearrange(
                "p (b c i t) -> p b c t i", c=BLOCK // PACK, i=PACK, t=PACK
            )
            in_ = rounded(c0, c1).rearrange("p b t (c i) -> p b c t i", i=PACK)
            copy(out=out[:, :, :, :planes], in_=in_[:, :, :, :planes])

        def place_last(copy, c0, c1):
            copy(
                out=out_grouped[:, c0 * PACK : c1 * PACK].rearrange("p (c t) -> p c t", t=PACK)[:, :, 3],
                in_=windows[3][:, c0:c1],
            )

        out_scale = keep.tile([P, QUARTER], U8, name="out_scale", align_bytes=ALIGN)
        code_tiles = [
            keep.tile([P, c1 - c0], I32, name=f"codes{c0}", align_bytes=ALIGN)
            for c0, c1 in zip(STORE_CUTS, STORE_CUTS[1:])
        ]

        def quantize_out(c0, c1):
            s, r = divmod(c0, QUARTER)
            tile, base = holder(code_tiles, STORE_CUTS, c0)
            nc.vector.quantize_mx(
                out=tile[:, c0 - base : c1 - base].bitcast(FP8X4),
                scales=out_scale[4 * s :, r : r + c1 - c0],
                in_=out_grouped[:, c0 * PACK : c1 * PACK],
            )

        def store_words(c0, queue=nc.sync):
            n = STORE_CUTS.index(c0)
            queue.dma_start(out_words[:, c0 : STORE_CUTS[n + 1]], code_tiles[n][:])

        vcopy = nc.vector.tensor_copy
        scopy = nc.scalar.copy
        round_plane(gpsimd_copy, 1, 0, T)
        round_plane(vcopy, 2, 0, 448)
        round_plane(gpsimd_copy, 2, 448, T)
        round_plane(scopy, 0, 0, 128)
        round_plane(scopy, 0, 128, 1280)
        round_plane(gpsimd_copy, 0, 1280, T)
        group(scopy, 0, 128, 3)

        place_last(scopy, 0, 128)
        round_plane(vcopy, 3, 128, 512)
        round_plane(vcopy, 3, 512, 1280)
        round_plane(vcopy, 3, 1280, T)
        for c0, c1 in [(128, 256), (256, 512), (1280, 1664), (1792, 1920), (1920, T)]:
            group(scopy, c0, c1)
        group(vcopy, 512, 768)
        group(vcopy, 768, 1024)
        quantize_out(0, 256)
        quantize_out(768, 1024)
        quantize_out(512, 768)
        quantize_out(256, 512)
        store_words(0)
        group(vcopy, 1024, 1280)
        group(vcopy, 1664, 1792)
        quantize_out(1024, 1280)
        quantize_out(1280, 1536)
        quantize_out(1536, 1664)
        store_words(1024)
        quantize_out(1664, 1792)
        quantize_out(1792, 1920)
        quantize_out(1920, T)
        store_words(1664, nc.scalar)

        for q in range(QUADS):
            nc.sync.dma_start(
                out_2[0, 4 * q : 4 * q + 4, :].bitcast(I32).rearrange("r (s c) -> s r c", s=QUADS),
                out_scale[32 * q : 32 * q + 16, :].bitcast(I32),
            )
